import numpy as np
import ml_dtypes


def mxq(x, axis, fmt="e4m3"):
    dtype, down = {"e4m3": (ml_dtypes.float8_e4m3fn, 7), "e5m2": (ml_dtypes.float8_e5m2, 14)}[fmt]
    v = np.moveaxis(np.asarray(x, np.float32).astype(ml_dtypes.bfloat16).astype(np.float64), axis, -1)
    blocks = v.reshape(v.shape[:-1] + (-1, 32))
    amax = np.abs(blocks).max(-1, keepdims=True)
    byte = np.maximum(np.where(amax > 0, np.frexp(amax)[1] - 1 + 127, 0) - down, 1)
    scale = np.exp2(byte - 127.0)
    codes = (blocks / scale).astype(np.float32).astype(dtype).astype(np.float64)
    return np.moveaxis((codes * scale).reshape(v.shape), -1, axis)


WIDE = False


def mx_kscale(k):
    if not WIDE:
        return np.ones(k)
    levels = np.array([10, -10, 5, -5, 0])
    if k % 512:
        return np.exp2(np.random.permutation(np.resize(levels, k // 32))).repeat(32)
    a = np.empty((k // 512, 16))
    for p in range(k // 512):
        a[p, :8] = np.random.permutation(np.resize(levels, 8))
        for g in range(8):
            far = levels[np.abs(levels - a[p, g]) >= 10]
            a[p, g + 8] = far[np.random.randint(len(far))]
    return np.exp2(a.ravel()).repeat(32)


def f64(x):
    return np.asarray(x).astype(np.float64)


def striped(idx):
    return np.tile(idx.reshape(-1, 16).T, (8, 1)).astype(np.uint16)


def unstriped(offs):
    return offs[:16].T.reshape(-1).astype(np.int64)


E2M1 = np.array([0.0, 0.5, 1.0, 1.5, 2.0, 3.0, 4.0, 6.0, -0.0, -0.5, -1.0, -1.5, -2.0, -3.0, -4.0, -6.0])


def pack_weight(w, fmt):
    k, n = w.shape
    w = f64(np.asarray(w, np.float32).astype(ml_dtypes.bfloat16)).reshape(k // 32, 32, n)
    amax = np.abs(w).max(1)
    if fmt == "e4m3":
        byte = np.frexp(amax)[1] - 1 + 127 - 7
    else:
        mant, ex = np.frexp(amax / 6.0)
        byte = np.where(mant > 0.5, ex, ex - 1) + 127
    byte = np.clip(np.where(amax > 0, byte, 1), 1, 254)
    scaled = (w * np.exp2(127.0 - byte)[:, None, :]).reshape(k, n).astype(np.float32)
    by_word = np.ascontiguousarray(scaled.reshape(k // 512, 128, 4, n).transpose(0, 1, 3, 2))
    if fmt == "e4m3":
        words = by_word.astype(ml_dtypes.float8_e4m3fn).view(np.uint8)
    else:
        c = by_word.astype(ml_dtypes.float4_e2m1fn).view(np.uint8) & 0xF
        words = (c[..., 0::2] | (c[..., 1::2] << 4)).reshape(k // 512, 128, 2 * n)
    return np.ascontiguousarray(words), np.ascontiguousarray(byte.astype(np.uint8).reshape(k // 512, 16, n))


def unpack_weight(words, scales, fmt):
    g, _, n = scales.shape
    words = np.ascontiguousarray(words).reshape(g, 128, n, -1)
    if fmt == "e4m3":
        vals = words.view(ml_dtypes.float8_e4m3fn).astype(np.float64)
    else:
        nib = np.empty((g, 128, n, 4), np.uint8)
        nib[..., 0::2] = words & 0xF
        nib[..., 1::2] = words >> 4
        vals = E2M1[nib]
    vals = vals * np.repeat(np.exp2(scales.astype(np.float64) - 127.0), 8, axis=1)[..., None]
    return vals.transpose(0, 1, 3, 2).reshape(g * 512, n)


def gelu(v):
    return 0.5 * v * (1.0 + np.tanh(np.sqrt(2.0 / np.pi) * (v + 0.044715 * v**3)))


K, T, E, C, H, N, TOP = 1024, 768, 12, 256, 512, 256, 4


def by_expert(wq, xq):
    return np.concatenate([wq[e].T @ xq[:, e * C:(e + 1) * C] for e in range(E)], axis=1)


def setup_inputs():
    n = np.random.standard_normal
    s = mx_kscale(K)
    u = mx_kscale(H)
    deal = np.repeat(np.arange(E), C).reshape(TOP, T)[:, np.random.permutation(T)]
    deal = np.take_along_axis(deal, np.argsort(np.random.rand(TOP, T), axis=0), axis=0)
    for _ in range(8):
        s_, t_ = np.random.permutation(T).reshape(2, -1); r = np.random.randint(TOP, size=T // 2); x, y = deal[r, s_].copy(), deal[r, t_].copy()
        ok = ~((deal[:, s_] == y).any(0) | (deal[:, t_] == x).any(0)); deal[r[ok], s_[ok]] = y[ok]; deal[r[ok], t_[ok]] = x[ok]
    order = np.lexsort((np.random.rand(TOP * T), deal.reshape(-1)))
    slot_token = order % T; pos = np.empty(TOP * T, np.int64); pos[order] = np.arange(TOP * T); pos = pos.reshape(TOP, T)
    g = np.random.uniform(0.5, 1.5, (TOP, T)); g = g / g.sum(0)
    x = pack_weight(n((K, T)) * s[:, None], "e4m3")
    w1 = pack_weight(n((K, H)) / np.sqrt(K) / s[:, None] * u, "e4m3")
    return {
        "x_words": x[0],
        "x_scales": x[1],
        "w1_words": w1[0],
        "w1_scales": w1[1],
        "w2": (n((E, H, N)) / np.sqrt(H) / u[None, :, None]).astype(np.float32),
        "gate": np.stack([np.tile(r, (128, 1)) for r in g]).astype(np.float32),
        "offs": striped(slot_token),
        "pos1": striped(pos[0]),
        "pos2": striped(pos[1]),
        "pos3": striped(pos[2]),
        "pos4": striped(pos[3]),
    }


def reference(x_words, x_scales, w1_words, w1_scales, w2, gate, offs, pos1, pos2, pos3, pos4):
    w1 = unpack_weight(w1_words, w1_scales, "e4m3")
    w2q = mxq(f64(w2), 1, "e4m3")
    idx = unstriped(offs)
    x = unpack_weight(x_words, x_scales, "e4m3")
    h = gelu(w1.T @ x)
    y = by_expert(w2q, mxq(h[:, idx], 0, "e4m3"))
    out = sum(f64(gate[r, :1]) * y[:, unstriped(p)] for r, p in enumerate((pos1, pos2, pos3, pos4)))
    return out

@@ -1,0 +1,230 @@
+from contextlib import ExitStack
+
+import concourse.mybir as mybir
+from concourse.masks import make_identity
+
+K, T, E, C, H, N, TOP = 1024, 768, 12, 256, 512, 256, 4
+S = E * C
+FLOPS = 2 * K * H * T + 2 * H * N * S
+
+F32 = mybir.dt.float32
+BF16 = mybir.dt.bfloat16
+I32 = mybir.dt.int32
+U32 = mybir.dt.uint32
+U16 = mybir.dt.uint16
+U8 = mybir.dt.uint8
+FP8X4 = mybir.dt.float8_e4m3fn_x4
+MULT = mybir.AluOpType.mult
+ADD = mybir.AluOpType.add
+GELU = mybir.ActivationFunctionType.Gelu_apprx_tanh
+
+P = 128
+PASSES = K // 512
+TOK = 256
+UNITS = [(0, 2), (2, 2), (4, 2), (6, 2), (8, 2), (10, 1), (11, 1)]
+VECTOR_CASTS = (0, 1, 2)
+VECTOR_INTERLEAVES = (6,)
+CASTS_IN_STEP = [(5, 6), (7, 8), (9,), (10,), (11,), (), ()]
+PIECES = [(0, 0, 256), (0, 256, 256), (0, 512, 256), (1, 0, 256), (1, 256, 256), (1, 512, 128), (1, 640, 128)]
+
+
+def tile_moe_sup_lin_gelu_kernel(
+    tc, x_words, x_scales, w1_words, w1_scales, w2, gate, offs, pos1, pos2, pos3, pos4, out
+):
+    nc = tc.nc
+    with ExitStack() as ctx:
+        lists = ctx.enter_context(tc.tile_pool(name="lists", bufs=1))
+        keep = ctx.enter_context(tc.tile_pool(name="keep", bufs=1))
+        ring = ctx.enter_context(tc.tile_pool(name="ring", bufs=4))
+        pair = ctx.enter_context(tc.tile_pool(name="pair", bufs=2))
+        psum = ctx.enter_context(tc.psum_pool(name="psum", bufs=8))
+
+        def held(shape, dtype, name):
+            return keep.tile(shape, dtype, name=name, align_bytes=64)
+
+        def passing(shape, dtype, name):
+            return ring.tile(shape, dtype, name=name, align_bytes=64)
+
+        def bank():
+            return psum.tile([P, 512], F32, name="bank")
+
+        offs_sb = lists.tile([P, S // 16], U16, name="offs_sb")
+        pos_sb = [lists.tile([P, T // 16], U16, name="pos_sb%d" % r) for r in range(TOP)]
+
+        w1_raw = held([P, PASSES, H], U32, "w1_raw")
+        w1s_raw = held([P, H], U8, "w1s_raw")
+        x_sb = held([P, PASSES, T], U32, "x_sb")
+        xs_sb = held([P, T], U8, "xs_sb")
+        nc.vector.memset(w1s_raw[:].bitcast(I32), 0)
+        nc.vector.memset(xs_sb[:].bitcast(I32), 0)
+
+        nc.sync.dma_start(w1_raw[:].bitcast(I32), w1_words.rearrange("s p i d -> p s (i d)").bitcast(I32))
+        for q in range(4):
+            nc.sync.dma_start(w1s_raw[32 * q : 32 * q + 8, :].bitcast(I32), w1_scales[:, 4 * q : 4 * q + 4, :].bitcast(I32))
+        x_rows = x_words.rearrange("s p t d -> p s (t d)").bitcast(I32)
+        nc.sync.dma_start(x_sb[:, :, 0:TOK].bitcast(I32), x_rows[:, :, 0:TOK])
+        for q in range(4):
+            nc.sync.dma_start(xs_sb[32 * q : 32 * q + 8, :].bitcast(I32), x_scales[:, 4 * q : 4 * q + 4, :].bitcast(I32))
+        nc.sync.dma_start(x_sb[:, :, TOK:T].bitcast(I32), x_rows[:, :, TOK:T])
+        nc.sync.dma_start(offs_sb[:], offs)
+        w2_raw = [held([P, 4, N], F32, "w2_raw%d" % e) for e in range(E)]
+        for e in range(E):
+            nc.sync.dma_start(w2_raw[e][:], w2[e].rearrange("(p j) n -> p j n", j=4))
+        for r, pos in enumerate((pos1, pos2, pos3, pos4)):
+            nc.sync.dma_start(pos_sb[r][:], pos)
+        gate_sb = held([P, TOP, T], F32, "gate_sb")
+        nc.sync.dma_start(gate_sb[:], gate.rearrange("r p t -> p r t"))
+
+        ident = held([P, P], F32, "ident")
+        make_identity(nc, ident[:])
+
+        w1s_sb = held([P, H], U8, "w1s_sb")
+        nc.vector.tensor_copy(w1s_sb[:].rearrange("p (j m) -> p j m", j=4), w1s_raw[:].rearrange("p (m j) -> p j m", j=4))
+        w1_sb = held([P, PASSES, 4, P], U32, "w1_sb")
+        for u in range(2):
+            nc.vector.tensor_copy(
+                w1_sb[:, :, 2 * u : 2 * u + 2, :].bitcast(I32),
+                w1_raw[:].bitcast(I32).rearrange("p s (m j) -> p s j m", j=4)[:, :, 2 * u : 2 * u + 2, :],
+            )
+
+        h_pairs = [held([P, T], U32, "h_pairs%d" % u) for u in range(2)]
+        for u in range(2):
+            for t0 in range(0, T, TOK):
+                acc = bank()
+                for d in range(2):
+                    j = 2 * u + d
+                    for s in range(PASSES):
+                        nc.tensor.matmul_mx(
+                            out=acc[:, d * TOK : (d + 1) * TOK],
+                            lhsT=w1_sb[:, s, j, :].bitcast(FP8X4),
+                            lhsT_scale=w1s_sb[4 * s : P, j * P : (j + 1) * P],
+                            rhs=x_sb[:, s, t0 : t0 + TOK].bitcast(FP8X4),
+                            rhs_scale=xs_sb[4 * s : P, t0 : t0 + TOK],
+                            start=(s == 0),
+                            stop=(s == PASSES - 1),
+                        )
+                nc.scalar.activation(
+                    h_pairs[u][:, t0 : t0 + TOK].bitcast(BF16).rearrange("p (t d) -> p t d", d=2),
+                    acc[:].rearrange("p (d t) -> p t d", d=2),
+                    GELU,
+                )
+
+        w2_codes = [held([P, N], U32, "w2_codes%d" % e) for e in range(E)]
+        w2_scales = [held([P, N], U8, "w2_scales%d" % e) for e in range(E)]
+        w2_bf = {}
+
+        def cast_w2(e):
+            w2_bf[e] = passing([P, 4 * N], BF16, "w2_bf")
+            dst = w2_bf[e][:].rearrange("p (c i j) -> p c j i", i=4, j=4)
+            src = w2_raw[e][:].rearrange("p j (c i) -> p c j i", i=4)
+            if e in VECTOR_CASTS:
+                nc.vector.tensor_copy(dst, src)
+            else:
+                nc.scalar.copy(dst, src)
+
+        def quantize_w2(e):
+            nc.vector.quantize_mx(out=w2_codes[e][:].bitcast(FP8X4), scales=w2_scales[e][:], in_=w2_bf[e][:])
+
+        units = len(UNITS)
+        picked = {}
+        h_bf = {}
+        sums = {}
+        y = [held([P, S], F32, "y%d" % half) for half in range(2)]
+
+        def gather_h(g):
+            first, count = UNITS[g]
+            picked[g] = pair.tile([P, 2, count * C], U32, name="picked", align_bytes=64)
+            cols = offs_sb[:, first * C // 16 : (first + count) * C // 16]
+            for u in range(2):
+                nc.vector.tensor_copy(picked[g][:, u, :], h_pairs[u][:].indirect(cols))
+
+        def interleave_h(g):
+            h_bf[g] = passing([P, 4 * UNITS[g][1] * C], BF16, "h_bf")
+            dst = h_bf[g][:].bitcast(F32).rearrange("p (s u) -> p s u", u=2)
+            src = picked[g][:].bitcast(F32).rearrange("p u s -> p s u")
+            if g in VECTOR_INTERLEAVES:
+                nc.vector.tensor_copy(dst, src)
+            else:
+                nc.scalar.copy(dst, src)
+
+        def second_layer(g):
+            first, count = UNITS[g]
+            h_codes = passing([P, count * C], U32, "h_codes")
+            h_scales = passing([P, count * C], U8, "h_scales")
+            nc.vector.quantize_mx(out=h_codes[:].bitcast(FP8X4), scales=h_scales[:], in_=h_bf[g][:])
+            for half in range(2):
+                sums[g, half] = bank()
+                for a in range(count):
+                    nc.tensor.matmul_mx(
+                        out=sums[g, half][:, a * C : (a + 1) * C],
+                        lhsT=w2_codes[first + a][:, half * P : (half + 1) * P].bitcast(FP8X4),
+                        lhsT_scale=w2_scales[first + a][:, half * P : (half + 1) * P],
+                        rhs=h_codes[:, a * C : (a + 1) * C].bitcast(FP8X4),
+                        rhs_scale=h_scales[:, a * C : (a + 1) * C],
+                        start=True,
+                        stop=True,
+                    )
+
+        def store_y(g):
+            first, count = UNITS[g]
+            for half in range(2):
+                nc.scalar.copy(y[half][:, first * C : (first + count) * C], sums[g, half][:, 0 : count * C])
+
+        gather_h(0)
+        for e in range(5):
+            cast_w2(e)
+            if e > 0:
+                quantize_w2(e - 1)
+        waiting = [4]
+        for g in range(units):
+            interleave_h(g)
+            if g + 1 < units:
+                gather_h(g + 1)
+            if g > 0:
+                store_y(g - 1)
+            for e in waiting:
+                quantize_w2(e)
+            second_layer(g)
+            waiting = CASTS_IN_STEP[g]
+            for e in waiting:
+                cast_w2(e)
+        store_y(units - 1)
+
+        for k, (half, t0, width) in enumerate(PIECES):
+            terms = held([P, TOP, width], F32, "terms%d" % k)
+            result = held([P, width], F32, "result%d" % k)
+
+            def gather_term(r):
+                nc.vector.tensor_tensor(
+                    terms[:, r, :],
+                    y[half][:].indirect(pos_sb[r][:, t0 // 16 : (t0 + width) // 16]),
+                    gate_sb[:, r, t0 : t0 + width],
+                    MULT,
+                )
+
+            if k + 1 < len(PIECES):
+                blocks = width // P
+                totals = [bank() for b in range(blocks)]
+                for r in range(TOP):
+                    gather_term(r)
+                    for b in range(blocks):
+                        nc.tensor.matmul(
+                            totals[b][:, 0:P], lhsT=terms[:, r, b * P : (b + 1) * P], rhs=ident[:],
+                            start=(r == 0), stop=(r == TOP - 1), is_transpose=True,
+                        )
+                turned = held([P, width], F32, "turned%d" % k)
+                back = bank()
+                for b in range(blocks):
+                    nc.scalar.copy(turned[:, b * P : (b + 1) * P], totals[b][:, 0:P])
+                    nc.tensor.transpose(back[:, b * P : (b + 1) * P], turned[:, b * P : (b + 1) * P], ident[:])
+                nc.scalar.copy(result[:], back[:, 0:width])
+            else:
+                part = held([P, 2, width], F32, "part")
+                gather_term(0)
+                gather_term(1)
+                gather_term(2)
+                nc.vector.tensor_tensor(part[:, 0, :], terms[:, 0, :], terms[:, 1, :], ADD)
+                gather_term(3)
+                nc.vector.tensor_tensor(part[:, 1, :], part[:, 0, :], terms[:, 2, :], ADD)
+                nc.vector.tensor_tensor(result[:], part[:, 1, :], terms[:, 3, :], ADD)
+            nc.sync.dma_start(out[half * P : (half + 1) * P, t0 : t0 + width], result[:])

@@ -22,10 +22,10 @@ P = 128
 PASSES = K // 512
 TOK = 256
 UNITS = [(0, 2), (2, 2), (4, 2), (6, 2), (8, 2), (10, 1), (11, 1)]
-VECTOR_CASTS = (0, 1, 2)
+VECTOR_CASTS = (0, 1)
+GPSIMD_CASTS = (3, 5, 7, 9, 11)
 VECTOR_INTERLEAVES = (6,)
-CASTS_IN_STEP = [(5, 6), (7, 8), (9,), (10,), (11,), (), ()]
-PIECES = [(0, 0, 256), (0, 256, 256), (0, 512, 256), (1, 0, 256), (1, 256, 256), (1, 512, 128), (1, 640, 128)]
+PIECES = [(0, 0, 384), (0, 384, 384), (1, 0, 384), (1, 384, 256), (1, 640, 128)]
 
 
 def tile_moe_sup_lin_gelu_kernel(
@@ -61,11 +61,10 @@ def tile_moe_sup_lin_gelu_kernel(
         nc.sync.dma_start(w1_raw[:].bitcast(I32), w1_words.rearrange("s p i d -> p s (i d)").bitcast(I32))
         for q in range(4):
             nc.sync.dma_start(w1s_raw[32 * q : 32 * q + 8, :].bitcast(I32), w1_scales[:, 4 * q : 4 * q + 4, :].bitcast(I32))
-        x_rows = x_words.rearrange("s p t d -> p s (t d)").bitcast(I32)
-        nc.sync.dma_start(x_sb[:, :, 0:TOK].bitcast(I32), x_rows[:, :, 0:TOK])
         for q in range(4):
+            if q == 2:
+                nc.sync.dma_start(x_sb[:].bitcast(I32), x_words.rearrange("s p t d -> p s (t d)").bitcast(I32))
             nc.sync.dma_start(xs_sb[32 * q : 32 * q + 8, :].bitcast(I32), x_scales[:, 4 * q : 4 * q + 4, :].bitcast(I32))
-        nc.sync.dma_start(x_sb[:, :, TOK:T].bitcast(I32), x_rows[:, :, TOK:T])
         nc.sync.dma_start(offs_sb[:], offs)
         w2_raw = [held([P, 4, N], F32, "w2_raw%d" % e) for e in range(E)]
         for e in range(E):
@@ -114,7 +113,15 @@ def tile_moe_sup_lin_gelu_kernel(
         w2_bf = {}
 
         def cast_w2(e):
-            w2_bf[e] = passing([P, 4 * N], BF16, "w2_bf")
+            if e in GPSIMD_CASTS or e == 1:
+                w2_bf[e] = held([P, 4 * N], BF16, "w2_bf_single")
+            else:
+                w2_bf[e] = passing([P, 4 * N], BF16, "w2_bf")
+            if e in GPSIMD_CASTS:
+                nc.gpsimd.tensor_scalar(
+                    w2_bf[e][:].rearrange("p (n j) -> p n j", j=4), w2_raw[e][:].rearrange("p j n -> p n j"), 1.0, 0.0, MULT, ADD
+                )
+                return
             dst = w2_bf[e][:].rearrange("p (c i j) -> p c j i", i=4, j=4)
             src = w2_raw[e][:].rearrange("p j (c i) -> p c j i", i=4)
             if e in VECTOR_CASTS:
@@ -170,24 +177,28 @@ def tile_moe_sup_lin_gelu_kernel(
             for half in range(2):
                 nc.scalar.copy(y[half][:, first * C : (first + count) * C], sums[g, half][:, 0 : count * C])
 
+        cast_w2(0)
+        cast_w2(1)
+        quantize_w2(0)
+        quantize_w2(1)
+        cast_w2(2)
+        cast_w2(3)
         gather_h(0)
-        for e in range(5):
-            cast_w2(e)
-            if e > 0:
-                quantize_w2(e - 1)
-        waiting = [4]
         for g in range(units):
+            if 2 * g + 3 < E:
+                quantize_w2(2 * g + 3)
+            if 2 * g + 5 < E:
+                cast_w2(2 * g + 5)
             interleave_h(g)
             if g + 1 < units:
                 gather_h(g + 1)
             if g > 0:
                 store_y(g - 1)
-            for e in waiting:
-                quantize_w2(e)
+            if 2 * g + 2 < E:
+                quantize_w2(2 * g + 2)
             second_layer(g)
-            waiting = CASTS_IN_STEP[g]
-            for e in waiting:
-                cast_w2(e)
+            if 2 * g + 4 < E:
+                cast_w2(2 * g + 4)
         store_y(units - 1)
 
         for k, (half, t0, width) in enumerate(PIECES):

@@ -21,10 +21,6 @@ GELU = mybir.ActivationFunctionType.Gelu_apprx_tanh
 P = 128
 PASSES = K // 512
 TOK = 256
-UNITS = [(0, 2), (2, 2), (4, 2), (6, 2), (8, 2), (10, 1), (11, 1)]
-VECTOR_CASTS = (0, 1)
-GPSIMD_CASTS = (3, 5, 7, 9, 11)
-VECTOR_INTERLEAVES = (6,)
 PIECES = [(0, 0, 384), (0, 384, 384), (1, 0, 384), (1, 384, 256), (1, 640, 128)]
 
 
@@ -108,98 +104,111 @@ def tile_moe_sup_lin_gelu_kernel(
                     GELU,
                 )
 
-        w2_codes = [held([P, N], U32, "w2_codes%d" % e) for e in range(E)]
-        w2_scales = [held([P, N], U8, "w2_scales%d" % e) for e in range(E)]
-        w2_bf = {}
+        pairs = E // 2
+        picked, staged, quantized, sums = {}, {}, {}, {}
+        y = [held([P, S], F32, "y%d" % half) for half in range(2)]
 
-        def cast_w2(e):
-            if e in GPSIMD_CASTS or e == 1:
-                w2_bf[e] = held([P, 4 * N], BF16, "w2_bf_single")
-            else:
-                w2_bf[e] = passing([P, 4 * N], BF16, "w2_bf")
-            if e in GPSIMD_CASTS:
-                nc.gpsimd.tensor_scalar(
-                    w2_bf[e][:].rearrange("p (n j) -> p n j", j=4), w2_raw[e][:].rearrange("p j n -> p n j"), 1.0, 0.0, MULT, ADD
-                )
+        def stage(key, words):
+            staged[key] = pair.tile([P, words, 4], BF16, name="staged", align_bytes=64)
+
+        def cast_w2(e, dst, engine):
+            if engine is nc.gpsimd:
+                nc.gpsimd.tensor_scalar(dst, w2_raw[e][:].rearrange("p j n -> p n j"), 1.0, 0.0, MULT, ADD)
                 return
-            dst = w2_bf[e][:].rearrange("p (c i j) -> p c j i", i=4, j=4)
+            dst = dst.rearrange("p (c i) j -> p c j i", i=4)
             src = w2_raw[e][:].rearrange("p j (c i) -> p c j i", i=4)
-            if e in VECTOR_CASTS:
+            if engine is nc.vector:
                 nc.vector.tensor_copy(dst, src)
             else:
                 nc.scalar.copy(dst, src)
 
-        def quantize_w2(e):
-            nc.vector.quantize_mx(out=w2_codes[e][:].bitcast(FP8X4), scales=w2_scales[e][:], in_=w2_bf[e][:])
-
-        units = len(UNITS)
-        picked = {}
-        h_bf = {}
-        sums = {}
-        y = [held([P, S], F32, "y%d" % half) for half in range(2)]
+        def quantize(key, names):
+            col0 = names[0][1]
+            words = len(names) * C
+            codes = passing([P, words], U32, "codes")
+            scales = passing([P, words], U8, "scales")
+            nc.vector.quantize_mx(
+                out=codes[:].bitcast(FP8X4),
+                scales=scales[:],
+                in_=staged[key][:, col0 : col0 + words, :].rearrange("p w j -> p (w j)"),
+            )
+            for name, col in names:
+                quantized[name] = (codes, scales, col - col0)
 
         def gather_h(g):
-            first, count = UNITS[g]
-            picked[g] = pair.tile([P, 2, count * C], U32, name="picked", align_bytes=64)
-            cols = offs_sb[:, first * C // 16 : (first + count) * C // 16]
+            picked[g] = pair.tile([P, 2, 2 * C], U32, name="picked", align_bytes=64)
+            cols = offs_sb[:, 2 * g * C // 16 : 2 * (g + 1) * C // 16]
             for u in range(2):
                 nc.vector.tensor_copy(picked[g][:, u, :], h_pairs[u][:].indirect(cols))
 
         def interleave_h(g):
-            h_bf[g] = passing([P, 4 * UNITS[g][1] * C], BF16, "h_bf")
-            dst = h_bf[g][:].bitcast(F32).rearrange("p (s u) -> p s u", u=2)
-            src = picked[g][:].bitcast(F32).rearrange("p u s -> p s u")
-            if g in VECTOR_INTERLEAVES:
-                nc.vector.tensor_copy(dst, src)
-            else:
-                nc.scalar.copy(dst, src)
+            nc.scalar.copy(
+                staged[g][:, 0 : 2 * C, :].rearrange("p s j -> p (s j)").bitcast(F32).rearrange("p (s u) -> p s u", u=2),
+                picked[g][:].bitcast(F32).rearrange("p u s -> p s u"),
+            )
 
-        def second_layer(g):
-            first, count = UNITS[g]
-            h_codes = passing([P, count * C], U32, "h_codes")
-            h_scales = passing([P, count * C], U8, "h_scales")
-            nc.vector.quantize_mx(out=h_codes[:].bitcast(FP8X4), scales=h_scales[:], in_=h_bf[g][:])
-            for half in range(2):
-                sums[g, half] = bank()
-                for a in range(count):
+        def second_layer(experts, halves=(0, 1)):
+            for half in halves:
+                sums[experts, half] = bank()
+                for a, e in enumerate(experts):
+                    w_codes, w_scales, w_col = quantized["w", e]
+                    h_codes, h_scales, h_col = quantized["h", e]
+                    w_cols = slice(w_col + half * P, w_col + (half + 1) * P)
                     nc.tensor.matmul_mx(
-                        out=sums[g, half][:, a * C : (a + 1) * C],
-                        lhsT=w2_codes[first + a][:, half * P : (half + 1) * P].bitcast(FP8X4),
-                        lhsT_scale=w2_scales[first + a][:, half * P : (half + 1) * P],
-                        rhs=h_codes[:, a * C : (a + 1) * C].bitcast(FP8X4),
-                        rhs_scale=h_scales[:, a * C : (a + 1) * C],
+                        out=sums[experts, half][:, a * C : (a + 1) * C],
+                        lhsT=w_codes[:, w_cols].bitcast(FP8X4),
+                        lhsT_scale=w_scales[:, w_cols],
+                        rhs=h_codes[:, h_col : h_col + C].bitcast(FP8X4),
+                        rhs_scale=h_scales[:, h_col : h_col + C],
                         start=True,
                         stop=True,
                     )
 
-        def store_y(g):
-            first, count = UNITS[g]
-            for half in range(2):
-                nc.scalar.copy(y[half][:, first * C : (first + count) * C], sums[g, half][:, 0 : count * C])
+        def store_y(experts, halves=(0, 1)):
+            for half in halves:
+                dst = y[half][:, experts[0] * C : (experts[-1] + 1) * C]
+                src = sums[experts, half][:, 0 : len(experts) * C]
+                if experts == (E - 1,) and half == 0:
+                    nc.vector.tensor_copy(dst, src)
+                else:
+                    nc.scalar.copy(dst, src)
 
-        cast_w2(0)
-        cast_w2(1)
-        quantize_w2(0)
-        quantize_w2(1)
-        cast_w2(2)
-        cast_w2(3)
+        def open_pair(g):
+            stage(g, 4 * C)
+            cast_w2(2 * g + 1, staged[g][:, 3 * C : 4 * C, :], nc.gpsimd)
+            cast_w2(2 * g, staged[g][:, 2 * C : 3 * C, :], nc.scalar)
+
+        stage("first", 2 * C)
+        for e in range(2):
+            cast_w2(e, staged["first"][:, e * C : (e + 1) * C, :], nc.vector)
+        quantize("first", [(("w", 0), 0), (("w", 1), C)])
+        stage(0, 2 * C)
+        open_pair(1)
         gather_h(0)
-        for g in range(units):
-            if 2 * g + 3 < E:
-                quantize_w2(2 * g + 3)
-            if 2 * g + 5 < E:
-                cast_w2(2 * g + 5)
+        for g in range(pairs):
+            a, b = 2 * g, 2 * g + 1
+            slots = [(("h", a), 0), (("h", b), C)]
+            weights = [(("w", a), 2 * C), (("w", b), 3 * C)]
             interleave_h(g)
-            if g + 1 < units:
+            if g + 1 < pairs:
                 gather_h(g + 1)
-            if g > 0:
-                store_y(g - 1)
-            if 2 * g + 2 < E:
-                quantize_w2(2 * g + 2)
-            second_layer(g)
-            if 2 * g + 4 < E:
-                cast_w2(2 * g + 4)
-        store_y(units - 1)
+            if g + 1 < pairs:
+                if g > 0:
+                    store_y((a - 2, b - 2))
+                quantize(g, slots + (weights if g > 0 else []))
+                second_layer((a, b), (0, 1) if g + 2 < pairs else (0,))
+            else:
+                store_y((a - 2, b - 2), (0,))
+                quantize(g, weights)
+                for e, slot in zip((a, b), slots):
+                    quantize(g, [slot])
+                    second_layer((e,), (0,))
+                    store_y((e,), (0,))
+                for experts in ((a - 2, b - 2), (a, b)):
+                    second_layer(experts, (1,))
+                    store_y(experts, (1,))
+            if g + 2 < pairs:
+                open_pair(g + 2)
 
         for k, (half, t0, width) in enumerate(PIECES):
             terms = held([P, TOP, width], F32, "terms%d" % k)

@@ -21,7 +21,7 @@ GELU = mybir.ActivationFunctionType.Gelu_apprx_tanh
 P = 128
 PASSES = K // 512
 TOK = 256
-PIECES = [(0, 0, 384), (0, 384, 384), (1, 0, 384), (1, 384, 256), (1, 640, 128)]
+PAIRS = E // 2
 
 
 def tile_moe_sup_lin_gelu_kernel(
@@ -31,18 +31,12 @@ def tile_moe_sup_lin_gelu_kernel(
     with ExitStack() as ctx:
         lists = ctx.enter_context(tc.tile_pool(name="lists", bufs=1))
         keep = ctx.enter_context(tc.tile_pool(name="keep", bufs=1))
-        ring = ctx.enter_context(tc.tile_pool(name="ring", bufs=4))
-        pair = ctx.enter_context(tc.tile_pool(name="pair", bufs=2))
-        psum = ctx.enter_context(tc.psum_pool(name="psum", bufs=8))
+        psum = ctx.enter_context(tc.psum_pool(name="psum", bufs=1))
 
-        def held(shape, dtype, name):
-            return keep.tile(shape, dtype, name=name, align_bytes=64)
+        def held(shape, dtype, name, tag=""):
+            return keep.tile(shape, dtype, name=name, tag=tag, align_bytes=64)
 
-        def passing(shape, dtype, name):
-            return ring.tile(shape, dtype, name=name, align_bytes=64)
-
-        def bank():
-            return psum.tile([P, 512], F32, name="bank")
+        banks = [psum.tile([P, 512], F32, name="bank%d" % b) for b in range(8)]
 
         offs_sb = lists.tile([P, S // 16], U16, name="offs_sb")
         pos_sb = [lists.tile([P, T // 16], U16, name="pos_sb%d" % r) for r in range(TOP)]
@@ -62,9 +56,12 @@ def tile_moe_sup_lin_gelu_kernel(
                 nc.sync.dma_start(x_sb[:].bitcast(I32), x_words.rearrange("s p t d -> p s (t d)").bitcast(I32))
             nc.sync.dma_start(xs_sb[32 * q : 32 * q + 8, :].bitcast(I32), x_scales[:, 4 * q : 4 * q + 4, :].bitcast(I32))
         nc.sync.dma_start(offs_sb[:], offs)
-        w2_raw = [held([P, 4, N], F32, "w2_raw%d" % e) for e in range(E)]
-        for e in range(E):
-            nc.sync.dma_start(w2_raw[e][:], w2[e].rearrange("(p j) n -> p j n", j=4))
+        w2_first = [held([P, 4, N], F32, "w2_first%d" % e) for e in range(2)]
+        for e in range(2):
+            nc.sync.dma_start(w2_first[e][:], w2[e].rearrange("(p j) n -> p j n", j=4))
+        w2_raw = {g: held([P, 2, 4, N], F32, "w2_raw%d" % g) for g in range(1, PAIRS)}
+        for g in range(1, PAIRS):
+            nc.sync.dma_start(w2_raw[g][:], w2[2 * g : 2 * g + 2].rearrange("e (p j) n -> p e j n", j=4))
         for r, pos in enumerate((pos1, pos2, pos3, pos4)):
             nc.sync.dma_start(pos_sb[r][:], pos)
         gate_sb = held([P, TOP, T], F32, "gate_sb")
@@ -85,7 +82,7 @@ def tile_moe_sup_lin_gelu_kernel(
         h_pairs = [held([P, T], U32, "h_pairs%d" % u) for u in range(2)]
         for u in range(2):
             for t0 in range(0, T, TOK):
-                acc = bank()
+                acc = banks[3 * u + t0 // TOK]
                 for d in range(2):
                     j = 2 * u + d
                     for s in range(PASSES):
@@ -104,147 +101,168 @@ def tile_moe_sup_lin_gelu_kernel(
                     GELU,
                 )
 
-        pairs = E // 2
-        picked, staged, quantized, sums = {}, {}, {}, {}
         y = [held([P, S], F32, "y%d" % half) for half in range(2)]
+        picked = [held([P, 2, 2 * C], U32, "picked%d" % b, "picked%d" % b) for b in range(2)]
+        staged = [held([P, 3 * C, 4], BF16, "staged%d" % b, "staged%d" % b) for b in range(2)]
+        late = held([P, (E - 2) * P, 4], BF16, "late")
+        quantized = {}
 
-        def stage(key, words):
-            staged[key] = pair.tile([P, words, 4], BF16, name="staged", align_bytes=64)
+        def quantize(src, names, tag=""):
+            words = sum(width for name, width in names)
+            label = "_".join(str(part) for part in names[0][0])
+            codes = held([P, words], U32, "codes_" + label, tag)[:]
+            scales = held([P, words], U8, "scales_" + label)
+            nc.vector.quantize_mx(out=codes.bitcast(FP8X4), scales=scales[:], in_=src.rearrange("p w j -> p (w j)"))
+            col = 0
+            for name, width in names:
+                quantized[name] = (codes[:, col : col + width], scales[:, col : col + width])
+                col = col + width
 
-        def cast_w2(e, dst, engine):
-            if engine is nc.gpsimd:
-                nc.gpsimd.tensor_scalar(dst, w2_raw[e][:].rearrange("p j n -> p n j"), 1.0, 0.0, MULT, ADD)
-                return
-            dst = dst.rearrange("p (c i) j -> p c j i", i=4)
-            src = w2_raw[e][:].rearrange("p j (c i) -> p c j i", i=4)
-            if engine is nc.vector:
-                nc.vector.tensor_copy(dst, src)
-            else:
-                nc.scalar.copy(dst, src)
-
-        def quantize(key, names):
-            col0 = names[0][1]
-            words = len(names) * C
-            codes = passing([P, words], U32, "codes")
-            scales = passing([P, words], U8, "scales")
-            nc.vector.quantize_mx(
-                out=codes[:].bitcast(FP8X4),
-                scales=scales[:],
-                in_=staged[key][:, col0 : col0 + words, :].rearrange("p w j -> p (w j)"),
-            )
-            for name, col in names:
-                quantized[name] = (codes, scales, col - col0)
-
-        def gather_h(g):
-            picked[g] = pair.tile([P, 2, 2 * C], U32, name="picked", align_bytes=64)
-            cols = offs_sb[:, 2 * g * C // 16 : 2 * (g + 1) * C // 16]
+        def gather_h(g, s0, width):
+            cols = offs_sb[:, (2 * g * C + s0) // 16 : (2 * g * C + s0 + width) // 16]
             for u in range(2):
-                nc.vector.tensor_copy(picked[g][:, u, :], h_pairs[u][:].indirect(cols))
+                nc.vector.tensor_copy(picked[g % 2][:, u, s0 : s0 + width], h_pairs[u][:].indirect(cols))
 
-        def interleave_h(g):
+        def interleave_h(g, s0, width):
             nc.scalar.copy(
-                staged[g][:, 0 : 2 * C, :].rearrange("p s j -> p (s j)").bitcast(F32).rearrange("p (s u) -> p s u", u=2),
-                picked[g][:].bitcast(F32).rearrange("p u s -> p s u"),
+                staged[g % 2][:, s0 : s0 + width, :].rearrange("p s j -> p (s j)").bitcast(F32).rearrange("p (s u) -> p s u", u=2),
+                picked[g % 2][:, :, s0 : s0 + width].bitcast(F32).rearrange("p u s -> p s u"),
             )
 
-        def second_layer(experts, halves=(0, 1)):
-            for half in halves:
-                sums[experts, half] = bank()
-                for a, e in enumerate(experts):
-                    w_codes, w_scales, w_col = quantized["w", e]
-                    h_codes, h_scales, h_col = quantized["h", e]
-                    w_cols = slice(w_col + half * P, w_col + (half + 1) * P)
-                    nc.tensor.matmul_mx(
-                        out=sums[experts, half][:, a * C : (a + 1) * C],
-                        lhsT=w_codes[:, w_cols].bitcast(FP8X4),
-                        lhsT_scale=w_scales[:, w_cols],
-                        rhs=h_codes[:, h_col : h_col + C].bitcast(FP8X4),
-                        rhs_scale=h_scales[:, h_col : h_col + C],
-                        start=True,
-                        stop=True,
-                    )
-
-        def store_y(experts, halves=(0, 1)):
-            for half in halves:
-                dst = y[half][:, experts[0] * C : (experts[-1] + 1) * C]
-                src = sums[experts, half][:, 0 : len(experts) * C]
-                if experts == (E - 1,) and half == 0:
-                    nc.vector.tensor_copy(dst, src)
-                else:
-                    nc.scalar.copy(dst, src)
-
-        def open_pair(g):
-            stage(g, 4 * C)
-            cast_w2(2 * g + 1, staged[g][:, 3 * C : 4 * C, :], nc.gpsimd)
-            cast_w2(2 * g, staged[g][:, 2 * C : 3 * C, :], nc.scalar)
-
-        stage("first", 2 * C)
-        for e in range(2):
-            cast_w2(e, staged["first"][:, e * C : (e + 1) * C, :], nc.vector)
-        quantize("first", [(("w", 0), 0), (("w", 1), C)])
-        stage(0, 2 * C)
-        open_pair(1)
-        gather_h(0)
-        for g in range(pairs):
-            a, b = 2 * g, 2 * g + 1
-            slots = [(("h", a), 0), (("h", b), C)]
-            weights = [(("w", a), 2 * C), (("w", b), 3 * C)]
-            interleave_h(g)
-            if g + 1 < pairs:
-                gather_h(g + 1)
-            if g + 1 < pairs:
-                if g > 0:
-                    store_y((a - 2, b - 2))
-                quantize(g, slots + (weights if g > 0 else []))
-                second_layer((a, b), (0, 1) if g + 2 < pairs else (0,))
-            else:
-                store_y((a - 2, b - 2), (0,))
-                quantize(g, weights)
-                for e, slot in zip((a, b), slots):
-                    quantize(g, [slot])
-                    second_layer((e,), (0,))
-                    store_y((e,), (0,))
-                for experts in ((a - 2, b - 2), (a, b)):
-                    second_layer(experts, (1,))
-                    store_y(experts, (1,))
-            if g + 2 < pairs:
-                open_pair(g + 2)
-
-        for k, (half, t0, width) in enumerate(PIECES):
-            terms = held([P, TOP, width], F32, "terms%d" % k)
-            result = held([P, width], F32, "result%d" % k)
-
-            def gather_term(r):
-                nc.vector.tensor_tensor(
-                    terms[:, r, :],
-                    y[half][:].indirect(pos_sb[r][:, t0 // 16 : (t0 + width) // 16]),
-                    gate_sb[:, r, t0 : t0 + width],
-                    MULT,
+        def second_layer(experts, half, bank):
+            for a, e in enumerate(experts):
+                w_codes, w_scales = quantized["w", e, half]
+                h_codes, h_scales = quantized["h", e]
+                nc.tensor.matmul_mx(
+                    out=bank[:, a * C : (a + 1) * C],
+                    lhsT=w_codes.bitcast(FP8X4),
+                    lhsT_scale=w_scales,
+                    rhs=h_codes.bitcast(FP8X4),
+                    rhs_scale=h_scales,
+                    start=True,
+                    stop=True,
                 )
 
-            if k + 1 < len(PIECES):
-                blocks = width // P
-                totals = [bank() for b in range(blocks)]
-                for r in range(TOP):
-                    gather_term(r)
-                    for b in range(blocks):
-                        nc.tensor.matmul(
-                            totals[b][:, 0:P], lhsT=terms[:, r, b * P : (b + 1) * P], rhs=ident[:],
-                            start=(r == 0), stop=(r == TOP - 1), is_transpose=True,
-                        )
-                turned = held([P, width], F32, "turned%d" % k)
-                back = bank()
-                for b in range(blocks):
-                    nc.scalar.copy(turned[:, b * P : (b + 1) * P], totals[b][:, 0:P])
-                    nc.tensor.transpose(back[:, b * P : (b + 1) * P], turned[:, b * P : (b + 1) * P], ident[:])
-                nc.scalar.copy(result[:], back[:, 0:width])
+        def store_y(experts, half, bank):
+            nc.scalar.copy(y[half][:, experts[0] * C : (experts[-1] + 1) * C], bank[:, 0 : len(experts) * C])
+
+        def cast_early(g):
+            nc.gpsimd.tensor_scalar(
+                staged[g % 2][:, 2 * C : 3 * C, :].rearrange("p (e n) j -> p e n j", e=2),
+                w2_raw[g][:, :, :, 0:P].rearrange("p e j n -> p e n j"),
+                1.0, 0.0, MULT, ADD,
+            )
+
+        def cast_late(g):
+            nc.scalar.copy(
+                late[:, (g - 1) * C : g * C, :].rearrange("p (e c i) j -> p e c j i", e=2, i=4),
+                w2_raw[g][:, :, :, P:N].rearrange("p e j (c i) -> p e c j i", i=4),
+            )
+
+        for e in range(2):
+            dst = staged[e][:, 2 * C : 3 * C, :]
+            nc.vector.tensor_copy(
+                dst.rearrange("p (c i) j -> p c j i", i=4), w2_first[e][:].rearrange("p j (c i) -> p c j i", i=4)
+            )
+            quantize(dst, [(("w", e, 0), P), (("w", e, 1), P)])
+
+        last = PAIRS - 1
+        cast_early(1)
+        gather_h(0, 0, 2 * C)
+        for g in range(last):
+            a, b = 2 * g, 2 * g + 1
+            interleave_h(g, 0, 2 * C)
+            if g + 1 < last:
+                gather_h(g + 1, 0, 2 * C)
             else:
-                part = held([P, 2, width], F32, "part")
-                gather_term(0)
-                gather_term(1)
-                gather_term(2)
-                nc.vector.tensor_tensor(part[:, 0, :], terms[:, 0, :], terms[:, 1, :], ADD)
-                gather_term(3)
-                nc.vector.tensor_tensor(part[:, 1, :], part[:, 0, :], terms[:, 2, :], ADD)
-                nc.vector.tensor_tensor(result[:], part[:, 1, :], terms[:, 3, :], ADD)
-            nc.sync.dma_start(out[half * P : (half + 1) * P, t0 : t0 + width], result[:])
+                gather_h(g + 1, 0, C)
+                gather_h(g + 1, C, C)
+            if g > 0:
+                store_y((a - 2, b - 2), 0, banks[6 + (g - 1) % 2])
+            if g == 1:
+                store_y((0, 1), 1, banks[0])
+            cast_late(g + 1)
+            if g == 0:
+                quantize(staged[0][:, 0 : 2 * C, :], [(("h", a), C), (("h", b), C)])
+            else:
+                quantize(staged[g % 2][:, 0:C, :], [(("h", a), C)])
+                quantize(staged[g % 2][:, C : 3 * C, :], [(("h", b), C), (("w", a, 0), P), (("w", b, 0), P)])
+            second_layer((a, b), 0, banks[6 + g % 2])
+            if g == 0:
+                second_layer((a, b), 1, banks[0])
+            if g + 2 <= last:
+                cast_early(g + 2)
+
+        a, b = E - 2, E - 1
+        tile = staged[last % 2]
+        interleave_h(last, 0, C)
+        interleave_h(last, C, C)
+        store_y((a - 2, b - 2), 0, banks[6 + (last - 1) % 2])
+        quantize(tile[:, 2 * C : 3 * C, :], [(("w", a, 0), P), (("w", b, 0), P)])
+        for k, e in enumerate((a, b)):
+            quantize(tile[:, k * C : (k + 1) * C, :], [(("h", e), C)])
+            second_layer((e,), 0, banks[1 + k])
+            store_y((e,), 0, banks[1 + k])
+
+        quantize(late[:, 0:C, :], [(("w", e, 1), P) for e in (2, 3)], "picked%d" % (last % 2))
+        quantize(late[:, C : 5 * C, :], [(("w", e, 1), P) for e in range(4, E)], "staged%d" % (last % 2))
+        for g in range(1, PAIRS):
+            second_layer((2 * g, 2 * g + 1), 1, banks[2 + g])
+            store_y((2 * g, 2 * g + 1), 1, banks[2 + g])
+
+        def gather_term(terms, r, half, t0, width):
+            nc.vector.tensor_tensor(
+                terms[:, r, :],
+                y[half][:].indirect(pos_sb[r][:, t0 // 16 : (t0 + width) // 16]),
+                gate_sb[:, r, t0 : t0 + width],
+                MULT,
+            )
+
+        def add_turned(total, terms, r, b):
+            nc.tensor.matmul(
+                total, lhsT=terms[:, r, b * P : (b + 1) * P], rhs=ident[:],
+                start=(r == 0), stop=(r == TOP - 1), is_transpose=True,
+            )
+
+        terms = held([P, TOP, T], F32, "terms_first")
+        turned = held([P, T], F32, "turned_first")
+        result = held([P, T], F32, "result_first")
+        for r in range(TOP):
+            gather_term(terms, r, 0, 0, T)
+        for k, (b0, b1) in enumerate(((0, 4), (4, 6))):
+            cols = slice(b0 * P, b1 * P)
+            width = (b1 - b0) * P
+            for b in range(b0, b1):
+                for r in range(TOP):
+                    add_turned(banks[k][:, (b - b0) * P : (b - b0 + 1) * P], terms, r, b)
+            nc.scalar.copy(turned[:, cols], banks[k][:, 0:width])
+            for b in range(b0, b1):
+                nc.tensor.transpose(banks[2 + k][:, (b - b0) * P : (b - b0 + 1) * P], turned[:, b * P : (b + 1) * P], ident[:])
+            nc.scalar.copy(result[:, cols], banks[2 + k][:, 0:width])
+        nc.scalar.dma_start(out[0:P, :], result[:])
+
+        for t0, width, totals, back in ((0, 3 * P, banks[4:7], banks[7]), (3 * P, 2 * P, banks[0:2], banks[2])):
+            terms = held([P, TOP, width], F32, "terms%d" % t0)
+            turned = held([P, width], F32, "turned%d" % t0)
+            result = held([P, width], F32, "result%d" % t0)
+            for r in range(TOP):
+                gather_term(terms, r, 1, t0, width)
+                for b in range(width // P):
+                    add_turned(totals[b][:, 0:P], terms, r, b)
+            for b in range(width // P):
+                nc.scalar.copy(turned[:, b * P : (b + 1) * P], totals[b][:, 0:P])
+                nc.tensor.transpose(back[:, b * P : (b + 1) * P], turned[:, b * P : (b + 1) * P], ident[:])
+            nc.scalar.copy(result[:], back[:, 0:width])
+            nc.scalar.dma_start(out[P:N, t0 : t0 + width], result[:])
+
+        t0 = T - P
+        terms = held([P, TOP, P], F32, "terms_last")
+        part = held([P, 2, P], F32, "part")
+        result = held([P, P], F32, "result_last")
+        for r in range(3):
+            gather_term(terms, r, 1, t0, P)
+        nc.vector.tensor_tensor(part[:, 0, :], terms[:, 0, :], terms[:, 1, :], ADD)
+        gather_term(terms, 3, 1, t0, P)
+        nc.vector.tensor_tensor(part[:, 1, :], part[:, 0, :], terms[:, 2, :], ADD)
+        nc.vector.tensor_tensor(result[:], part[:, 1, :], terms[:, 3, :], ADD)
+        nc.sync.dma_start(out[P:N, t0:T], result[:])

@@ -20,7 +20,7 @@ GELU = mybir.ActivationFunctionType.Gelu_apprx_tanh
 
 P = 128
 PASSES = K // 512
-TOK = 256
+CHUNKS = ((0, 256), (256, 256), (512, 128), (640, 128))
 PAIRS = E // 2
 
 
@@ -42,19 +42,23 @@ def tile_moe_sup_lin_gelu_kernel(
         pos_sb = [lists.tile([P, T // 16], U16, name="pos_sb%d" % r) for r in range(TOP)]
 
         w1_raw = held([P, PASSES, H], U32, "w1_raw")
-        w1s_raw = held([P, H], U8, "w1s_raw")
+        w1s_raw = held([P, PASSES, H], U8, "w1s_raw")
         x_sb = held([P, PASSES, T], U32, "x_sb")
-        xs_sb = held([P, T], U8, "xs_sb")
-        nc.vector.memset(w1s_raw[:].bitcast(I32), 0)
-        nc.vector.memset(xs_sb[:].bitcast(I32), 0)
+        xs_sb = held([P, PASSES, T], U8, "xs_sb")
+        nc.vector.memset(w1s_raw[:].rearrange("p s n -> p (s n)").bitcast(I32), 0)
+        nc.vector.memset(xs_sb[:].rearrange("p s n -> p (s n)").bitcast(I32), 0)
+
+        def load_scales(plane, first, scales, r):
+            rows = scales.rearrange("s (q r) n -> r q s n", r=4)[r]
+            nc.sync.dma_start(plane[first + r : P : 32, :, :].bitcast(I32), rows.bitcast(I32))
 
         nc.sync.dma_start(w1_raw[:].bitcast(I32), w1_words.rearrange("s p i d -> p s (i d)").bitcast(I32))
-        for q in range(4):
-            nc.sync.dma_start(w1s_raw[32 * q : 32 * q + 8, :].bitcast(I32), w1_scales[:, 4 * q : 4 * q + 4, :].bitcast(I32))
-        for q in range(4):
-            if q == 2:
+        for r in range(4):
+            load_scales(w1s_raw, 0, w1_scales, r)
+        for r in range(4):
+            if r == 2:
                 nc.sync.dma_start(x_sb[:].bitcast(I32), x_words.rearrange("s p t d -> p s (t d)").bitcast(I32))
-            nc.sync.dma_start(xs_sb[32 * q : 32 * q + 8, :].bitcast(I32), x_scales[:, 4 * q : 4 * q + 4, :].bitcast(I32))
+            load_scales(xs_sb, 4, x_scales, r)
         nc.sync.dma_start(offs_sb[:], offs)
         w2_first = [held([P, 4, N], F32, "w2_first%d" % e) for e in range(2)]
         for e in range(2):
@@ -70,10 +74,13 @@ def tile_moe_sup_lin_gelu_kernel(
         ident = held([P, P], F32, "ident")
         make_identity(nc, ident[:])
 
-        w1s_sb = held([P, H], U8, "w1s_sb")
-        nc.vector.tensor_copy(w1s_sb[:].rearrange("p (j m) -> p j m", j=4), w1s_raw[:].rearrange("p (m j) -> p j m", j=4))
+        w1s_sb = held([P, PASSES, H], U8, "w1s_sb")
         w1_sb = held([P, PASSES, 4, P], U32, "w1_sb")
         for u in range(2):
+            nc.vector.tensor_copy(
+                w1s_sb[:].rearrange("p s (j m) -> p s j m", j=4)[:, :, 2 * u : 2 * u + 2, :],
+                w1s_raw[:].rearrange("p s (m j) -> p s j m", j=4)[:, :, 2 * u : 2 * u + 2, :],
+            )
             nc.vector.tensor_copy(
                 w1_sb[:, :, 2 * u : 2 * u + 2, :].bitcast(I32),
                 w1_raw[:].bitcast(I32).rearrange("p s (m j) -> p s j m", j=4)[:, :, 2 * u : 2 * u + 2, :],
@@ -81,30 +88,31 @@ def tile_moe_sup_lin_gelu_kernel(
 
         h_pairs = [held([P, T], U32, "h_pairs%d" % u) for u in range(2)]
         for u in range(2):
-            for t0 in range(0, T, TOK):
-                acc = banks[3 * u + t0 // TOK]
+            for k, (t0, width) in enumerate(CHUNKS):
+                acc = banks[len(CHUNKS) * u + k]
                 for d in range(2):
                     j = 2 * u + d
                     for s in range(PASSES):
                         nc.tensor.matmul_mx(
-                            out=acc[:, d * TOK : (d + 1) * TOK],
+                            out=acc[:, d * width : (d + 1) * width],
                             lhsT=w1_sb[:, s, j, :].bitcast(FP8X4),
-                            lhsT_scale=w1s_sb[4 * s : P, j * P : (j + 1) * P],
-                            rhs=x_sb[:, s, t0 : t0 + TOK].bitcast(FP8X4),
-                            rhs_scale=xs_sb[4 * s : P, t0 : t0 + TOK],
+                            lhsT_scale=w1s_sb[:, s, j * P : (j + 1) * P],
+                            rhs=x_sb[:, s, t0 : t0 + width].bitcast(FP8X4),
+                            rhs_scale=xs_sb[4:P, s, t0 : t0 + width],
                             start=(s == 0),
                             stop=(s == PASSES - 1),
                         )
                 nc.scalar.activation(
-                    h_pairs[u][:, t0 : t0 + TOK].bitcast(BF16).rearrange("p (t d) -> p t d", d=2),
-                    acc[:].rearrange("p (d t) -> p t d", d=2),
+                    h_pairs[u][:, t0 : t0 + width].bitcast(BF16).rearrange("p (t d) -> p t d", d=2),
+                    acc[:, 0 : 2 * width].rearrange("p (d t) -> p t d", d=2),
                     GELU,
                 )
 
         y = [held([P, S], F32, "y%d" % half) for half in range(2)]
         picked = [held([P, 2, 2 * C], U32, "picked%d" % b, "picked%d" % b) for b in range(2)]
         staged = [held([P, 3 * C, 4], BF16, "staged%d" % b, "staged%d" % b) for b in range(2)]
-        late = held([P, (E - 2) * P, 4], BF16, "late")
+        staged_first = held([P, 2 * C, 4], BF16, "staged_first", "late_a")
+        late = held([P, 4 * C, 4], BF16, "late")
         quantized = {}
 
         def quantize(src, names, tag=""):
@@ -124,8 +132,9 @@ def tile_moe_sup_lin_gelu_kernel(
                 nc.vector.tensor_copy(picked[g % 2][:, u, s0 : s0 + width], h_pairs[u][:].indirect(cols))
 
         def interleave_h(g, s0, width):
+            dst = staged[g % 2] if g > 0 else staged_first
             nc.scalar.copy(
-                staged[g % 2][:, s0 : s0 + width, :].rearrange("p s j -> p (s j)").bitcast(F32).rearrange("p (s u) -> p s u", u=2),
+                dst[:, s0 : s0 + width, :].rearrange("p s j -> p (s j)").bitcast(F32).rearrange("p (s u) -> p s u", u=2),
                 picked[g % 2][:, :, s0 : s0 + width].bitcast(F32).rearrange("p u s -> p s u"),
             )
 
@@ -146,16 +155,19 @@ def tile_moe_sup_lin_gelu_kernel(
         def store_y(experts, half, bank):
             nc.scalar.copy(y[half][:, experts[0] * C : (experts[-1] + 1) * C], bank[:, 0 : len(experts) * C])
 
-        def cast_early(g):
+        def cast_gpsimd(g, half, dst):
             nc.gpsimd.tensor_scalar(
-                staged[g % 2][:, 2 * C : 3 * C, :].rearrange("p (e n) j -> p e n j", e=2),
-                w2_raw[g][:, :, :, 0:P].rearrange("p e j n -> p e n j"),
+                dst.rearrange("p (e n) j -> p e n j", e=2),
+                w2_raw[g][:, :, :, half * P : (half + 1) * P].rearrange("p e j n -> p e n j"),
                 1.0, 0.0, MULT, ADD,
             )
 
+        def cast_early(g):
+            cast_gpsimd(g, 0, staged[g % 2][:, 2 * C : 3 * C, :])
+
         def cast_late(g):
             nc.scalar.copy(
-                late[:, (g - 1) * C : g * C, :].rearrange("p (e c i) j -> p e c j i", e=2, i=4),
+                late[:, (g - 2) * C : (g - 1) * C, :].rearrange("p (e c i) j -> p e c j i", e=2, i=4),
                 w2_raw[g][:, :, :, P:N].rearrange("p e j (c i) -> p e c j i", i=4),
             )
 
@@ -179,19 +191,19 @@ def tile_moe_sup_lin_gelu_kernel(
                 gather_h(g + 1, C, C)
             if g > 0:
                 store_y((a - 2, b - 2), 0, banks[6 + (g - 1) % 2])
-            if g == 1:
-                store_y((0, 1), 1, banks[0])
-            cast_late(g + 1)
+            if g + 2 <= last:
+                cast_late(g + 2)
             if g == 0:
-                quantize(staged[0][:, 0 : 2 * C, :], [(("h", a), C), (("h", b), C)])
+                quantize(staged_first[:], [(("h", a), C), (("h", b), C)])
             else:
                 quantize(staged[g % 2][:, 0:C, :], [(("h", a), C)])
                 quantize(staged[g % 2][:, C : 3 * C, :], [(("h", b), C), (("w", a, 0), P), (("w", b, 0), P)])
             second_layer((a, b), 0, banks[6 + g % 2])
-            if g == 0:
-                second_layer((a, b), 1, banks[0])
             if g + 2 <= last:
                 cast_early(g + 2)
+            if g == 0:
+                late_a = held([P, C, 4], BF16, "late_a", "late_a")
+                cast_gpsimd(1, 1, late_a[:])
 
         a, b = E - 2, E - 1
         tile = staged[last % 2]
@@ -204,9 +216,9 @@ def tile_moe_sup_lin_gelu_kernel(
             second_layer((e,), 0, banks[1 + k])
             store_y((e,), 0, banks[1 + k])
 
-        quantize(late[:, 0:C, :], [(("w", e, 1), P) for e in (2, 3)], "picked%d" % (last % 2))
-        quantize(late[:, C : 5 * C, :], [(("w", e, 1), P) for e in range(4, E)], "staged%d" % (last % 2))
-        for g in range(1, PAIRS):
+        quantize(late_a[:], [(("w", e, 1), P) for e in (2, 3)], "picked%d" % (last % 2))
+        quantize(late[:], [(("w", e, 1), P) for e in range(4, E)], "staged%d" % (last % 2))
+        for g in range(PAIRS):
             second_layer((2 * g, 2 * g + 1), 1, banks[2 + g])
             store_y((2 * g, 2 * g + 1), 1, banks[2 + g])
 
@@ -229,16 +241,18 @@ def tile_moe_sup_lin_gelu_kernel(
         result = held([P, T], F32, "result_first")
         for r in range(TOP):
             gather_term(terms, r, 0, 0, T)
-        for k, (b0, b1) in enumerate(((0, 4), (4, 6))):
-            cols = slice(b0 * P, b1 * P)
-            width = (b1 - b0) * P
+            for b in range(2):
+                add_turned(banks[b][:, 0:P], terms, r, b)
+        for b in range(2):
+            nc.scalar.copy(turned[:, b * P : (b + 1) * P], banks[b][:, 0:P])
+        for b in range(2, 6):
+            for r in range(TOP):
+                add_turned(banks[2][:, (b - 2) * P : (b - 1) * P], terms, r, b)
+        nc.scalar.copy(turned[:, 2 * P : T], banks[2][:])
+        for back, b0, b1 in ((banks[0], 0, 2), (banks[3], 2, 6)):
             for b in range(b0, b1):
-                for r in range(TOP):
-                    add_turned(banks[k][:, (b - b0) * P : (b - b0 + 1) * P], terms, r, b)
-            nc.scalar.copy(turned[:, cols], banks[k][:, 0:width])
-            for b in range(b0, b1):
-                nc.tensor.transpose(banks[2 + k][:, (b - b0) * P : (b - b0 + 1) * P], turned[:, b * P : (b + 1) * P], ident[:])
-            nc.scalar.copy(result[:, cols], banks[2 + k][:, 0:width])
+                nc.tensor.transpose(back[:, (b - b0) * P : (b - b0 + 1) * P], turned[:, b * P : (b + 1) * P], ident[:])
+            nc.scalar.copy(result[:, b0 * P : b1 * P], back[:, 0 : (b1 - b0) * P])
         nc.scalar.dma_start(out[0:P, :], result[:])
 
         for t0, width, totals, back in ((0, 3 * P, banks[4:7], banks[7]), (3 * P, 2 * P, banks[0:2], banks[2])):

@@ -43,7 +43,7 @@ def tile_moe_sup_lin_gelu_kernel(
 
         w1_raw = held([P, PASSES, H], U32, "w1_raw")
         w1s_raw = held([P, PASSES, H], U8, "w1s_raw")
-        x_sb = held([P, PASSES, T], U32, "x_sb")
+        x_sb = held([P, PASSES, T], U32, "x_sb", "x_sb")
         xs_sb = held([P, PASSES, T], U8, "xs_sb")
         nc.vector.memset(w1s_raw[:].rearrange("p s n -> p (s n)").bitcast(I32), 0)
         nc.vector.memset(xs_sb[:].rearrange("p s n -> p (s n)").bitcast(I32), 0)
@@ -59,10 +59,10 @@ def tile_moe_sup_lin_gelu_kernel(
             if r == 2:
                 nc.sync.dma_start(x_sb[:].bitcast(I32), x_words.rearrange("s p t d -> p s (t d)").bitcast(I32))
             load_scales(xs_sb, 4, x_scales, r)
-        nc.sync.dma_start(offs_sb[:], offs)
         w2_first = [held([P, 4, N], F32, "w2_first%d" % e) for e in range(2)]
         for e in range(2):
             nc.sync.dma_start(w2_first[e][:], w2[e].rearrange("(p j) n -> p j n", j=4))
+        nc.sync.dma_start(offs_sb[:], offs)
         w2_raw = {g: held([P, 2, 4, N], F32, "w2_raw%d" % g) for g in range(1, PAIRS)}
         for g in range(1, PAIRS):
             nc.sync.dma_start(w2_raw[g][:], w2[2 * g : 2 * g + 2].rearrange("e (p j) n -> p e j n", j=4))
@@ -84,6 +84,17 @@ def tile_moe_sup_lin_gelu_kernel(
             nc.vector.tensor_copy(
                 w1_sb[:, :, 2 * u : 2 * u + 2, :].bitcast(I32),
                 w1_raw[:].bitcast(I32).rearrange("p s (m j) -> p s j m", j=4)[:, :, 2 * u : 2 * u + 2, :],
+            )
+
+        for s in range(PASSES):
+            nc.tensor.matmul_mx(
+                out=banks[7][:],
+                lhsT=w1_raw[:, s, 0:P].bitcast(FP8X4),
+                lhsT_scale=w1s_raw[:, s, 0:P],
+                rhs=w1_raw[:, s, :].bitcast(FP8X4),
+                rhs_scale=w1s_raw[:, s, :],
+                start=True,
+                stop=True,
             )
 
         h_pairs = [held([P, T], U32, "h_pairs%d" % u) for u in range(2)]
@@ -111,7 +122,7 @@ def tile_moe_sup_lin_gelu_kernel(
         y = [held([P, S], F32, "y%d" % half) for half in range(2)]
         picked = [held([P, 2, 2 * C], U32, "picked%d" % b, "picked%d" % b) for b in range(2)]
         staged = [held([P, 3 * C, 4], BF16, "staged%d" % b, "staged%d" % b) for b in range(2)]
-        staged_first = held([P, 2 * C, 4], BF16, "staged_first", "late_a")
+        late_a = held([P, C, 4], BF16, "late_a")
         late = held([P, 4 * C, 4], BF16, "late")
         quantized = {}
 
@@ -132,7 +143,7 @@ def tile_moe_sup_lin_gelu_kernel(
                 nc.vector.tensor_copy(picked[g % 2][:, u, s0 : s0 + width], h_pairs[u][:].indirect(cols))
 
         def interleave_h(g, s0, width):
-            dst = staged[g % 2] if g > 0 else staged_first
+            dst = staged[g % 2]
             nc.scalar.copy(
                 dst[:, s0 : s0 + width, :].rearrange("p s j -> p (s j)").bitcast(F32).rearrange("p (s u) -> p s u", u=2),
                 picked[g % 2][:, :, s0 : s0 + width].bitcast(F32).rearrange("p u s -> p s u"),
@@ -171,15 +182,28 @@ def tile_moe_sup_lin_gelu_kernel(
                 w2_raw[g][:, :, :, P:N].rearrange("p e j (c i) -> p e c j i", i=4),
             )
 
-        for e in range(2):
-            dst = staged[e][:, 2 * C : 3 * C, :]
-            nc.vector.tensor_copy(
-                dst.rearrange("p (c i) j -> p c j i", i=4), w2_first[e][:].rearrange("p j (c i) -> p c j i", i=4)
+        def cast_first(e, n0, n1, dst, copy):
+            copy(
+                dst.rearrange("p (c i) j -> p c j i", i=4),
+                w2_first[e][:, :, n0:n1].rearrange("p j (c i) -> p c j i", i=4),
             )
-            quantize(dst, [(("w", e, 0), P), (("w", e, 1), P)])
+
+        cast_first(0, 0, N, staged[0][:, 2 * C : 3 * C, :], nc.vector.tensor_copy)
+        quantize(staged[0][:, 2 * C : 3 * C, :], [(("w", 0, 0), P), (("w", 0, 1), P)])
+        cast_first(1, 0, P, staged[1][:, 2 * C : 2 * C + P, :], nc.vector.tensor_copy)
+        quantize(staged[1][:, 2 * C : 2 * C + P, :], [(("w", 1, 0), P)])
+        late_first = held([P, P, 4], BF16, "late_first", "x_sb")
+        cast_first(1, P, N, late_first[:], nc.scalar.copy)
 
         last = PAIRS - 1
         cast_early(1)
+        nc.gpsimd.tensor_scalar(
+            late_a[:, 0:P, :], w2_raw[1][:, 0, :, P:N].rearrange("p j n -> p n j"), 1.0, 0.0, MULT, ADD
+        )
+        nc.scalar.copy(
+            late_a[:, P:C, :].rearrange("p (c i) j -> p c j i", i=4),
+            w2_raw[1][:, 1, :, P:N].rearrange("p j (c i) -> p c j i", i=4),
+        )
         gather_h(0, 0, 2 * C)
         for g in range(last):
             a, b = 2 * g, 2 * g + 1
@@ -194,23 +218,22 @@ def tile_moe_sup_lin_gelu_kernel(
             if g + 2 <= last:
                 cast_late(g + 2)
             if g == 0:
-                quantize(staged_first[:], [(("h", a), C), (("h", b), C)])
+                quantize(staged[0][:, 0 : 2 * C, :], [(("h", a), C), (("h", b), C)])
+                staged[0] = held([P, 3 * C, 4], BF16, "staged_again", "staged0")
             else:
                 quantize(staged[g % 2][:, 0:C, :], [(("h", a), C)])
                 quantize(staged[g % 2][:, C : 3 * C, :], [(("h", b), C), (("w", a, 0), P), (("w", b, 0), P)])
             second_layer((a, b), 0, banks[6 + g % 2])
             if g + 2 <= last:
                 cast_early(g + 2)
-            if g == 0:
-                late_a = held([P, C, 4], BF16, "late_a", "late_a")
-                cast_gpsimd(1, 1, late_a[:])
+
 
         a, b = E - 2, E - 1
         tile = staged[last % 2]
         interleave_h(last, 0, C)
         interleave_h(last, C, C)
         store_y((a - 2, b - 2), 0, banks[6 + (last - 1) % 2])
-        quantize(tile[:, 2 * C : 3 * C, :], [(("w", a, 0), P), (("w", b, 0), P)])
+        quantize(tile[:, 2 * C : 3 * C, :], [(("w", a, 0), P), (("w", b, 0), P)], "last_codes")
         for k, e in enumerate((a, b)):
             quantize(tile[:, k * C : (k + 1) * C, :], [(("h", e), C)])
             second_layer((e,), 0, banks[1 + k])
@@ -218,7 +241,8 @@ def tile_moe_sup_lin_gelu_kernel(
 
         quantize(late_a[:], [(("w", e, 1), P) for e in (2, 3)], "picked%d" % (last % 2))
         quantize(late[:], [(("w", e, 1), P) for e in range(4, E)], "staged%d" % (last % 2))
-        for g in range(PAIRS):
+        quantize(late_first[:], [(("w", 1, 1), P)], "last_codes")
+        for g in (1, 2, 3, 4, 5, 0):
             second_layer((2 * g, 2 * g + 1), 1, banks[2 + g])
             store_y((2 * g, 2 * g + 1), 1, banks[2 + g])
 

@@ -22,6 +22,9 @@ P = 128
 PASSES = K // 512
 CHUNKS = ((0, 256), (256, 256), (512, 128), (640, 128))
 PAIRS = E // 2
+WINDOW = 2048
+GATHERS = ((0, 3), (3, 5), (5, 6))
+UNITS = ((0, 2), (2, 4), (4, 5), (5, 6))
 
 
 def tile_moe_sup_lin_gelu_kernel(
@@ -31,10 +34,14 @@ def tile_moe_sup_lin_gelu_kernel(
     with ExitStack() as ctx:
         lists = ctx.enter_context(tc.tile_pool(name="lists", bufs=1))
         keep = ctx.enter_context(tc.tile_pool(name="keep", bufs=1))
+        shared = ctx.enter_context(tc.tile_pool(name="shared", bufs=1))
         psum = ctx.enter_context(tc.psum_pool(name="psum", bufs=1))
 
         def held(shape, dtype, name, tag=""):
             return keep.tile(shape, dtype, name=name, tag=tag, align_bytes=64)
+
+        def placed(shape, dtype, name, offset):
+            return shared.tile(shape, dtype, name=name, offset=offset, align_bytes=64)
 
         banks = [psum.tile([P, 512], F32, name="bank%d" % b) for b in range(8)]
 
@@ -59,13 +66,19 @@ def tile_moe_sup_lin_gelu_kernel(
             if r == 2:
                 nc.sync.dma_start(x_sb[:].bitcast(I32), x_words.rearrange("s p t d -> p s (t d)").bitcast(I32))
             load_scales(xs_sb, 4, x_scales, r)
-        w2_first = [held([P, 4, N], F32, "w2_first%d" % e) for e in range(2)]
-        for e in range(2):
-            nc.sync.dma_start(w2_first[e][:], w2[e].rearrange("(p j) n -> p j n", j=4))
+        w2_first = [held([P, 2, 4, P], F32, "w2_first%d" % half) for half in range(2)]
+
+        def load_first(half):
+            for e in range(2):
+                nc.sync.dma_start(w2_first[half][:, e, :, :], w2[e].rearrange("(p j) n -> p j n", j=4)[:, :, half * P : (half + 1) * P])
+
+        load_first(0)
         nc.sync.dma_start(offs_sb[:], offs)
-        w2_raw = {g: held([P, 2, 4, N], F32, "w2_raw%d" % g) for g in range(1, PAIRS)}
+        w2_raw = {g: held([P, 2, 4, N], F32, "w2_raw%d" % g, "w2_raw%d" % g) for g in range(2, PAIRS)}
+        w2_raw[1] = placed([P, 2, 4, N], F32, "w2_raw1", 0)
         for g in range(1, PAIRS):
             nc.sync.dma_start(w2_raw[g][:], w2[2 * g : 2 * g + 2].rearrange("e (p j) n -> p e j n", j=4))
+        load_first(1)
         for r, pos in enumerate((pos1, pos2, pos3, pos4)):
             nc.sync.dma_start(pos_sb[r][:], pos)
         gate_sb = held([P, TOP, T], F32, "gate_sb")
@@ -97,7 +110,9 @@ def tile_moe_sup_lin_gelu_kernel(
                 stop=True,
             )
 
-        h_pairs = [held([P, T], U32, "h_pairs%d" % u) for u in range(2)]
+        h_pairs = [held([P, WINDOW], U32, "h_pairs%d" % u) for u in range(2)]
+        for u in range(2):
+            nc.vector.memset(h_pairs[u][:, T:WINDOW], 0)
         for u in range(2):
             for k, (t0, width) in enumerate(CHUNKS):
                 acc = banks[len(CHUNKS) * u + k]
@@ -119,40 +134,27 @@ def tile_moe_sup_lin_gelu_kernel(
                     GELU,
                 )
 
-        y = [held([P, S], F32, "y%d" % half) for half in range(2)]
-        picked = [held([P, 2, 2 * C], U32, "picked%d" % b, "picked%d" % b) for b in range(2)]
-        staged = [held([P, 3 * C, 4], BF16, "staged%d" % b, "staged%d" % b) for b in range(2)]
-        late_a = held([P, C, 4], BF16, "late_a")
-        late = held([P, 4 * C, 4], BF16, "late")
+        y = [placed([P, S], F32, "y0", 2048), held([P, S], F32, "y1")]
         quantized = {}
 
-        def quantize(src, names, tag=""):
+        def quantize(src, names, offset=None):
             words = sum(width for name, width in names)
             label = "_".join(str(part) for part in names[0][0])
-            codes = held([P, words], U32, "codes_" + label, tag)[:]
-            scales = held([P, words], U8, "scales_" + label)
+            codes = held([P, words], U32, "codes_" + label)[:]
+            if offset is None:
+                scales = held([P, words], U8, "scales_" + label)
+            else:
+                scales = placed([P, words], U8, "scales_" + label, offset)
             nc.vector.quantize_mx(out=codes.bitcast(FP8X4), scales=scales[:], in_=src.rearrange("p w j -> p (w j)"))
             col = 0
             for name, width in names:
                 quantized[name] = (codes[:, col : col + width], scales[:, col : col + width])
                 col = col + width
 
-        def gather_h(g, s0, width):
-            cols = offs_sb[:, (2 * g * C + s0) // 16 : (2 * g * C + s0 + width) // 16]
-            for u in range(2):
-                nc.vector.tensor_copy(picked[g % 2][:, u, s0 : s0 + width], h_pairs[u][:].indirect(cols))
-
-        def interleave_h(g, s0, width):
-            dst = staged[g % 2]
-            nc.scalar.copy(
-                dst[:, s0 : s0 + width, :].rearrange("p s j -> p (s j)").bitcast(F32).rearrange("p (s u) -> p s u", u=2),
-                picked[g % 2][:, :, s0 : s0 + width].bitcast(F32).rearrange("p u s -> p s u"),
-            )
-
-        def second_layer(experts, half, bank):
-            for a, e in enumerate(experts):
-                w_codes, w_scales = quantized["w", e, half]
-                h_codes, h_scales = quantized["h", e]
+        def second_layer(g, half, bank):
+            for a in range(2):
+                w_codes, w_scales = quantized["w", 2 * g + a, half]
+                h_codes, h_scales = quantized["h", 2 * g + a]
                 nc.tensor.matmul_mx(
                     out=bank[:, a * C : (a + 1) * C],
                     lhsT=w_codes.bitcast(FP8X4),
@@ -162,9 +164,7 @@ def tile_moe_sup_lin_gelu_kernel(
                     start=True,
                     stop=True,
                 )
-
-        def store_y(experts, half, bank):
-            nc.scalar.copy(y[half][:, experts[0] * C : (experts[-1] + 1) * C], bank[:, 0 : len(experts) * C])
+            nc.scalar.copy(y[half][:, 2 * g * C : (2 * g + 2) * C], bank[:])
 
         def cast_gpsimd(g, half, dst):
             nc.gpsimd.tensor_scalar(
@@ -173,134 +173,130 @@ def tile_moe_sup_lin_gelu_kernel(
                 1.0, 0.0, MULT, ADD,
             )
 
-        def cast_early(g):
-            cast_gpsimd(g, 0, staged[g % 2][:, 2 * C : 3 * C, :])
-
-        def cast_late(g):
-            nc.scalar.copy(
-                late[:, (g - 2) * C : (g - 1) * C, :].rearrange("p (e c i) j -> p e c j i", e=2, i=4),
-                w2_raw[g][:, :, :, P:N].rearrange("p e j (c i) -> p e c j i", i=4),
-            )
-
-        def cast_first(e, n0, n1, dst, copy):
+        def cast_runs(src, dst, copy):
             copy(
-                dst.rearrange("p (c i) j -> p c j i", i=4),
-                w2_first[e][:, :, n0:n1].rearrange("p j (c i) -> p c j i", i=4),
+                dst.rearrange("p (e c i) j -> p e c j i", e=2, i=4),
+                src.rearrange("p e j (c i) -> p e c j i", i=4),
             )
 
-        cast_first(0, 0, N, staged[0][:, 2 * C : 3 * C, :], nc.vector.tensor_copy)
-        quantize(staged[0][:, 2 * C : 3 * C, :], [(("w", 0, 0), P), (("w", 0, 1), P)])
-        cast_first(1, 0, P, staged[1][:, 2 * C : 2 * C + P, :], nc.vector.tensor_copy)
-        quantize(staged[1][:, 2 * C : 2 * C + P, :], [(("w", 1, 0), P)])
-        late_first = held([P, P, 4], BF16, "late_first", "x_sb")
-        cast_first(1, P, N, late_first[:], nc.scalar.copy)
+        def cast_scalar(g, dst):
+            cast_runs(w2_raw[g][:, :, :, P:N], dst, nc.scalar.copy)
 
-        last = PAIRS - 1
-        cast_early(1)
-        nc.gpsimd.tensor_scalar(
-            late_a[:, 0:P, :], w2_raw[1][:, 0, :, P:N].rearrange("p j n -> p n j"), 1.0, 0.0, MULT, ADD
-        )
-        nc.scalar.copy(
-            late_a[:, P:C, :].rearrange("p (c i) j -> p c j i", i=4),
-            w2_raw[1][:, 1, :, P:N].rearrange("p j (c i) -> p c j i", i=4),
-        )
-        gather_h(0, 0, 2 * C)
-        for g in range(last):
-            a, b = 2 * g, 2 * g + 1
-            interleave_h(g, 0, 2 * C)
-            if g + 1 < last:
-                gather_h(g + 1, 0, 2 * C)
-            else:
-                gather_h(g + 1, 0, C)
-                gather_h(g + 1, C, C)
-            if g > 0:
-                store_y((a - 2, b - 2), 0, banks[6 + (g - 1) % 2])
-            if g + 2 <= last:
-                cast_late(g + 2)
-            if g == 0:
-                quantize(staged[0][:, 0 : 2 * C, :], [(("h", a), C), (("h", b), C)])
-                staged[0] = held([P, 3 * C, 4], BF16, "staged_again", "staged0")
-            else:
-                quantize(staged[g % 2][:, 0:C, :], [(("h", a), C)])
-                quantize(staged[g % 2][:, C : 3 * C, :], [(("h", b), C), (("w", a, 0), P), (("w", b, 0), P)])
-            second_layer((a, b), 0, banks[6 + g % 2])
-            if g + 2 <= last:
-                cast_early(g + 2)
+        def quantize_w(src, pairs, half, offset=None):
+            quantize(src, [(("w", 2 * g + a, half), P) for g in pairs for a in range(2)], offset)
 
+        early_0 = held([P, C, 4], BF16, "early_0")
+        cast_runs(w2_first[0][:], early_0[:], nc.vector.tensor_copy)
+        quantize_w(early_0[:], (0,), 0)
 
-        a, b = E - 2, E - 1
-        tile = staged[last % 2]
-        interleave_h(last, 0, C)
-        interleave_h(last, C, C)
-        store_y((a - 2, b - 2), 0, banks[6 + (last - 1) % 2])
-        quantize(tile[:, 2 * C : 3 * C, :], [(("w", a, 0), P), (("w", b, 0), P)], "last_codes")
-        for k, e in enumerate((a, b)):
-            quantize(tile[:, k * C : (k + 1) * C, :], [(("h", e), C)])
-            second_layer((e,), 0, banks[1 + k])
-            store_y((e,), 0, banks[1 + k])
+        early_14 = held([P, 4 * C, 4], BF16, "early_14")
+        early_5 = held([P, C, 4], BF16, "early_5")
+        late_14 = held([P, 4 * C, 4], BF16, "late_14")
+        late_50 = held([P, 2 * C, 4], BF16, "late_50")
+        cast_gpsimd(1, 0, early_14[:, 0:C, :])
+        cast_gpsimd(2, 0, early_14[:, C : 2 * C, :])
+        cast_gpsimd(3, 0, early_14[:, 2 * C : 3 * C, :])
+        cast_gpsimd(3, 1, late_14[:, 2 * C : 3 * C, :])
+        cast_gpsimd(4, 0, early_14[:, 3 * C : 4 * C, :])
+        cast_gpsimd(5, 0, early_5[:])
+        cast_gpsimd(5, 1, late_50[:, 0:C, :])
+        cast_scalar(1, late_14[:, 0:C, :])
+        cast_scalar(2, late_14[:, C : 2 * C, :])
+        cast_scalar(4, late_14[:, 3 * C : 4 * C, :])
 
-        quantize(late_a[:], [(("w", e, 1), P) for e in (2, 3)], "picked%d" % (last % 2))
-        quantize(late[:], [(("w", e, 1), P) for e in range(4, E)], "staged%d" % (last % 2))
-        quantize(late_first[:], [(("w", 1, 1), P)], "last_codes")
+        picked = [held([P, 2, S // 2], U32, "picked0", "picked0"), placed([P, 2, S // 2], U32, "picked1", 0)]
+        for g0, g1 in GATHERS:
+            for u in range(2):
+                nc.vector.tensor_copy(
+                    picked[g0 // 3][:, u, g0 % 3 * 2 * C : (g0 % 3 + g1 - g0) * 2 * C],
+                    h_pairs[u][:].indirect(offs_sb[:, g0 * 2 * C // 16 : g1 * 2 * C // 16]),
+                )
+        staged = {}
+        for (g0, g1), tag in zip(UNITS, ("w2_raw2", "w2_raw4", "picked0", "w2_raw5")):
+            tile = held([P, (g1 - g0) * 2 * C, 4], BF16, "staged%d" % g0, tag)
+            for g in range(g0, g1):
+                staged[g] = (tile, g0)
+
+        def interleave_h(g0, g1):
+            dst, d0 = staged[g0]
+            nc.scalar.copy(
+                dst[:, (g0 - d0) * 2 * C : (g1 - d0) * 2 * C, :].rearrange("p s j -> p (s j)").bitcast(F32).rearrange("p (s u) -> p s u", u=2),
+                picked[g0 // 3][:, :, g0 % 3 * 2 * C : (g0 % 3 + g1 - g0) * 2 * C].bitcast(F32).rearrange("p u s -> p s u"),
+            )
+
+        for g0, g1 in ((0, 2), (2, 3), (3, 4), (4, 5)):
+            interleave_h(g0, g1)
+        cast_runs(w2_first[1][:], late_50[:, C : 2 * C, :], nc.scalar.copy)
+        interleave_h(5, 6)
+
+        def quantize_h(g0, g1):
+            quantize(staged[g0][0][:], [(("h", e), C) for e in range(2 * g0, 2 * g1)])
+
+        quantize_h(0, 2)
+        second_layer(0, 0, banks[0])
+        quantize_w(early_14[:], (1, 2, 3, 4), 0)
+        second_layer(1, 0, banks[1])
+        quantize_w(early_5[:], (5,), 0)
+        quantize_h(2, 4)
+        second_layer(2, 0, banks[2])
+        second_layer(3, 0, banks[3])
+        quantize_h(4, 5)
+        second_layer(4, 0, banks[4])
+        quantize_h(5, 6)
+        second_layer(5, 0, banks[5])
+        quantize_w(late_14[:], (1, 2, 3, 4), 1, 0)
+        quantize_w(late_50[:], (5, 0), 1, 1024)
         for g in (1, 2, 3, 4, 5, 0):
-            second_layer((2 * g, 2 * g + 1), 1, banks[2 + g])
-            store_y((2 * g, 2 * g + 1), 1, banks[2 + g])
+            second_layer(g, 1, banks[2 + (g + 3) % 6])
 
-        def gather_term(terms, r, half, t0, width):
+        def gather_term(term, r, half, t0, width):
             nc.vector.tensor_tensor(
-                terms[:, r, :],
+                term[:, t0 : t0 + width],
                 y[half][:].indirect(pos_sb[r][:, t0 // 16 : (t0 + width) // 16]),
                 gate_sb[:, r, t0 : t0 + width],
                 MULT,
             )
 
-        def add_turned(total, terms, r, b):
-            nc.tensor.matmul(
-                total, lhsT=terms[:, r, b * P : (b + 1) * P], rhs=ident[:],
-                start=(r == 0), stop=(r == TOP - 1), is_transpose=True,
-            )
-
-        terms = held([P, TOP, T], F32, "terms_first")
-        turned = held([P, T], F32, "turned_first")
-        result = held([P, T], F32, "result_first")
-        for r in range(TOP):
-            gather_term(terms, r, 0, 0, T)
-            for b in range(2):
-                add_turned(banks[b][:, 0:P], terms, r, b)
-        for b in range(2):
-            nc.scalar.copy(turned[:, b * P : (b + 1) * P], banks[b][:, 0:P])
-        for b in range(2, 6):
-            for r in range(TOP):
-                add_turned(banks[2][:, (b - 2) * P : (b - 1) * P], terms, r, b)
-        nc.scalar.copy(turned[:, 2 * P : T], banks[2][:])
-        for back, b0, b1 in ((banks[0], 0, 2), (banks[3], 2, 6)):
+        def add_turned(bank, term, b0, b1, first, last):
             for b in range(b0, b1):
-                nc.tensor.transpose(back[:, (b - b0) * P : (b - b0 + 1) * P], turned[:, b * P : (b + 1) * P], ident[:])
-            nc.scalar.copy(result[:, b0 * P : b1 * P], back[:, 0 : (b1 - b0) * P])
+                nc.tensor.matmul(
+                    bank[:, (b - b0) * P : (b - b0 + 1) * P], lhsT=term[:, b * P : (b + 1) * P], rhs=ident[:],
+                    start=(first and b == b0), stop=(last and b == b1 - 1), is_transpose=True,
+                )
+
+        def turn_back(total, back, b0, b1, name):
+            turned = held([P, (b1 - b0) * P], F32, "turned" + name)
+            nc.scalar.copy(turned[:], total[:, 0 : (b1 - b0) * P])
+            for b in range(b1 - b0):
+                nc.tensor.transpose(back[:, b * P : (b + 1) * P], turned[:, b * P : (b + 1) * P], ident[:])
+
+        terms = held([P, TOP, T], F32, "terms_first", "picked0")
+        result = held([P, T], F32, "result_first", "w2_raw5")
+        for r in range(TOP):
+            gather_term(terms[:, r, :], r, 0, 0, T)
+            add_turned(banks[0], terms[:, r, :], 0, 3, r == 0, r == TOP - 1)
+            add_turned(banks[1], terms[:, r, :], 3, 6, r == 0, r == TOP - 1)
+        for k in range(2):
+            turn_back(banks[k], banks[2 + k], 3 * k, 3 * k + 3, "first%d" % k)
+        for k in range(2):
+            nc.scalar.copy(result[:, 3 * k * P : (3 * k + 3) * P], banks[2 + k][:, 0 : 3 * P])
         nc.scalar.dma_start(out[0:P, :], result[:])
 
-        for t0, width, totals, back in ((0, 3 * P, banks[4:7], banks[7]), (3 * P, 2 * P, banks[0:2], banks[2])):
-            terms = held([P, TOP, width], F32, "terms%d" % t0)
-            turned = held([P, width], F32, "turned%d" % t0)
-            result = held([P, width], F32, "result%d" % t0)
-            for r in range(TOP):
-                gather_term(terms, r, 1, t0, width)
-                for b in range(width // P):
-                    add_turned(totals[b][:, 0:P], terms, r, b)
-            for b in range(width // P):
-                nc.scalar.copy(turned[:, b * P : (b + 1) * P], totals[b][:, 0:P])
-                nc.tensor.transpose(back[:, b * P : (b + 1) * P], turned[:, b * P : (b + 1) * P], ident[:])
-            nc.scalar.copy(result[:], back[:, 0:width])
-            nc.scalar.dma_start(out[P:N, t0 : t0 + width], result[:])
-
-        t0 = T - P
-        terms = held([P, TOP, P], F32, "terms_last")
-        part = held([P, 2, P], F32, "part")
-        result = held([P, P], F32, "result_last")
-        for r in range(3):
-            gather_term(terms, r, 1, t0, P)
-        nc.vector.tensor_tensor(part[:, 0, :], terms[:, 0, :], terms[:, 1, :], ADD)
-        gather_term(terms, 3, 1, t0, P)
-        nc.vector.tensor_tensor(part[:, 1, :], part[:, 0, :], terms[:, 2, :], ADD)
-        nc.vector.tensor_tensor(result[:], part[:, 1, :], terms[:, 3, :], ADD)
-        nc.sync.dma_start(out[P:N, t0:T], result[:])
+        terms = held([P, TOP, T], F32, "terms_second", "w2_raw3")
+        for r in range(TOP - 1):
+            gather_term(terms[:, r, :], r, 1, 0, T)
+            add_turned(banks[4], terms[:, r, :], 2, 6, r == 0, r == TOP - 2)
+            add_turned(banks[5], terms[:, r, :], 0, 2, r == 0, False)
+        turn_back(banks[4], banks[6], 2, 6, "second_b")
+        r = TOP - 1
+        for t0 in range(0, T, C):
+            gather_term(terms[:, r, :], r, 1, t0, C)
+        add_turned(banks[5], terms[:, r, :], 0, 2, False, True)
+        turn_back(banks[5], banks[7], 0, 2, "second_a")
+        result = held([P, C], F32, "result_a")
+        nc.scalar.copy(result[:], banks[7][:, 0:C])
+        nc.scalar.dma_start(out[P:N, 0:C], result[:])
+        for k in range(1, 3):
+            result = held([P, C], F32, "result_b%d" % k)
+            nc.vector.tensor_tensor(result[:], terms[:, r, k * C : (k + 1) * C], banks[6][:, (k - 1) * C : k * C], ADD)
+            nc.sync.dma_start(out[P:N, k * C : (k + 1) * C], result[:])

@@ -66,19 +66,14 @@ def tile_moe_sup_lin_gelu_kernel(
             if r == 2:
                 nc.sync.dma_start(x_sb[:].bitcast(I32), x_words.rearrange("s p t d -> p s (t d)").bitcast(I32))
             load_scales(xs_sb, 4, x_scales, r)
-        w2_first = [held([P, 2, 4, P], F32, "w2_first%d" % half) for half in range(2)]
-
-        def load_first(half):
-            for e in range(2):
-                nc.sync.dma_start(w2_first[half][:, e, :, :], w2[e].rearrange("(p j) n -> p j n", j=4)[:, :, half * P : (half + 1) * P])
-
-        load_first(0)
+        w2_first = [held([P, 4, N], F32, "w2_first%d" % e) for e in range(2)]
+        for e in range(2):
+            nc.sync.dma_start(w2_first[e][:], w2[e].rearrange("(p j) n -> p j n", j=4))
         nc.sync.dma_start(offs_sb[:], offs)
         w2_raw = {g: held([P, 2, 4, N], F32, "w2_raw%d" % g, "w2_raw%d" % g) for g in range(2, PAIRS)}
         w2_raw[1] = placed([P, 2, 4, N], F32, "w2_raw1", 0)
         for g in range(1, PAIRS):
             nc.sync.dma_start(w2_raw[g][:], w2[2 * g : 2 * g + 2].rearrange("e (p j) n -> p e j n", j=4))
-        load_first(1)
         for r, pos in enumerate((pos1, pos2, pos3, pos4)):
             nc.sync.dma_start(pos_sb[r][:], pos)
         gate_sb = held([P, TOP, T], F32, "gate_sb")
@@ -185,24 +180,31 @@ def tile_moe_sup_lin_gelu_kernel(
         def quantize_w(src, pairs, half, offset=None):
             quantize(src, [(("w", 2 * g + a, half), P) for g in pairs for a in range(2)], offset)
 
-        early_0 = held([P, C, 4], BF16, "early_0")
-        cast_runs(w2_first[0][:], early_0[:], nc.vector.tensor_copy)
-        quantize_w(early_0[:], (0,), 0)
+        def cast_first(e, n0, n1, dst, copy):
+            copy(
+                dst.rearrange("p (c i) j -> p c j i", i=4),
+                w2_first[e][:, :, n0:n1].rearrange("p j (c i) -> p c j i", i=4),
+            )
+
+        first_a = held([P, N, 4], BF16, "first_a")
+        first_b = held([P, P, 4], BF16, "first_b")
+        cast_first(0, 0, N, first_a[:], nc.vector.tensor_copy)
+        quantize(first_a[:], [(("w", 0, 0), P), (("w", 0, 1), P)])
+        cast_first(1, 0, P, first_b[:], nc.vector.tensor_copy)
+        quantize(first_b[:], [(("w", 1, 0), P)])
+        late_first = held([P, P, 4], BF16, "late_first", "x_sb")
+        cast_first(1, P, N, late_first[:], nc.scalar.copy)
 
         early_14 = held([P, 4 * C, 4], BF16, "early_14")
         early_5 = held([P, C, 4], BF16, "early_5")
         late_14 = held([P, 4 * C, 4], BF16, "late_14")
-        late_50 = held([P, 2 * C, 4], BF16, "late_50")
-        cast_gpsimd(1, 0, early_14[:, 0:C, :])
-        cast_gpsimd(2, 0, early_14[:, C : 2 * C, :])
-        cast_gpsimd(3, 0, early_14[:, 2 * C : 3 * C, :])
-        cast_gpsimd(3, 1, late_14[:, 2 * C : 3 * C, :])
-        cast_gpsimd(4, 0, early_14[:, 3 * C : 4 * C, :])
+        late_5 = held([P, C, 4], BF16, "late_5")
+        for g in range(1, 5):
+            cast_gpsimd(g, 0, early_14[:, (g - 1) * C : g * C, :])
         cast_gpsimd(5, 0, early_5[:])
-        cast_gpsimd(5, 1, late_50[:, 0:C, :])
-        cast_scalar(1, late_14[:, 0:C, :])
-        cast_scalar(2, late_14[:, C : 2 * C, :])
-        cast_scalar(4, late_14[:, 3 * C : 4 * C, :])
+        cast_gpsimd(5, 1, late_5[:])
+        for g in range(1, 5):
+            cast_scalar(g, late_14[:, (g - 1) * C : g * C, :])
 
         picked = [held([P, 2, S // 2], U32, "picked0", "picked0"), placed([P, 2, S // 2], U32, "picked1", 0)]
         for g0, g1 in GATHERS:
@@ -212,7 +214,7 @@ def tile_moe_sup_lin_gelu_kernel(
                     h_pairs[u][:].indirect(offs_sb[:, g0 * 2 * C // 16 : g1 * 2 * C // 16]),
                 )
         staged = {}
-        for (g0, g1), tag in zip(UNITS, ("w2_raw2", "w2_raw4", "picked0", "w2_raw5")):
+        for (g0, g1), tag in zip(UNITS, ("w2_raw3", "w2_raw4", "picked0", "w2_raw5")):
             tile = held([P, (g1 - g0) * 2 * C, 4], BF16, "staged%d" % g0, tag)
             for g in range(g0, g1):
                 staged[g] = (tile, g0)
@@ -224,10 +226,8 @@ def tile_moe_sup_lin_gelu_kernel(
                 picked[g0 // 3][:, :, g0 % 3 * 2 * C : (g0 % 3 + g1 - g0) * 2 * C].bitcast(F32).rearrange("p u s -> p s u"),
             )
 
-        for g0, g1 in ((0, 2), (2, 3), (3, 4), (4, 5)):
+        for g0, g1 in ((0, 2), (2, 3), (3, 4), (4, 5), (5, 6)):
             interleave_h(g0, g1)
-        cast_runs(w2_first[1][:], late_50[:, C : 2 * C, :], nc.scalar.copy)
-        interleave_h(5, 6)
 
         def quantize_h(g0, g1):
             quantize(staged[g0][0][:], [(("h", e), C) for e in range(2 * g0, 2 * g1)])
@@ -245,7 +245,8 @@ def tile_moe_sup_lin_gelu_kernel(
         quantize_h(5, 6)
         second_layer(5, 0, banks[5])
         quantize_w(late_14[:], (1, 2, 3, 4), 1, 0)
-        quantize_w(late_50[:], (5, 0), 1, 1024)
+        quantize_w(late_5[:], (5,), 1, 1024)
+        quantize(late_first[:], [(("w", 1, 1), P)], 1280)
         for g in (1, 2, 3, 4, 5, 0):
             second_layer(g, 1, banks[2 + (g + 3) % 6])
 
@@ -283,20 +284,22 @@ def tile_moe_sup_lin_gelu_kernel(
         nc.scalar.dma_start(out[0:P, :], result[:])
 
         terms = held([P, TOP, T], F32, "terms_second", "w2_raw3")
-        for r in range(TOP - 1):
+        for r in range(2):
             gather_term(terms[:, r, :], r, 1, 0, T)
-            add_turned(banks[4], terms[:, r, :], 2, 6, r == 0, r == TOP - 2)
-            add_turned(banks[5], terms[:, r, :], 0, 2, r == 0, False)
-        turn_back(banks[4], banks[6], 2, 6, "second_b")
-        r = TOP - 1
-        for t0 in range(0, T, C):
-            gather_term(terms[:, r, :], r, 1, t0, C)
-        add_turned(banks[5], terms[:, r, :], 0, 2, False, True)
-        turn_back(banks[5], banks[7], 0, 2, "second_a")
-        result = held([P, C], F32, "result_a")
-        nc.scalar.copy(result[:], banks[7][:, 0:C])
-        nc.scalar.dma_start(out[P:N, 0:C], result[:])
+            for k in range(3):
+                add_turned(banks[4 + k], terms[:, r, :], 2 * k, 2 * k + 2, r == 0, False)
+        gather_term(terms[:, 2, :], 2, 1, 0, C)
+        gather_term(terms[:, 2, :], 2, 1, C, 2 * C)
+        backs = (banks[7], banks[0], banks[1])
+        add_turned(banks[4], terms[:, 2, :], 0, 2, False, True)
+        turn_back(banks[4], backs[0], 0, 2, "second0")
         for k in range(1, 3):
-            result = held([P, C], F32, "result_b%d" % k)
-            nc.vector.tensor_tensor(result[:], terms[:, r, k * C : (k + 1) * C], banks[6][:, (k - 1) * C : k * C], ADD)
+            add_turned(banks[4 + k], terms[:, 2, :], 2 * k, 2 * k + 2, False, True)
+        for k in range(1, 3):
+            turn_back(banks[4 + k], backs[k], 2 * k, 2 * k + 2, "second%d" % k)
+        for k in range(3):
+            gather_term(terms[:, 3, :], 3, 1, k * C, C)
+        for k in range(3):
+            result = held([P, C], F32, "result_second%d" % k)
+            nc.vector.tensor_tensor(result[:], terms[:, 3, k * C : (k + 1) * C], backs[k][:, 0:C], ADD)
             nc.sync.dma_start(out[P:N, k * C : (k + 1) * C], result[:])

@@ -22,9 +22,8 @@ P = 128
 PASSES = K // 512
 CHUNKS = ((0, 256), (256, 256), (512, 128), (640, 128))
 PAIRS = E // 2
-WINDOW = 2048
-GATHERS = ((0, 3), (3, 5), (5, 6))
-UNITS = ((0, 2), (2, 4), (4, 5), (5, 6))
+WINDOW = 1536
+GATHERS = ((0, 2), (2, 4), (4, 5), (5, 6))
 
 
 def tile_moe_sup_lin_gelu_kernel(
@@ -70,10 +69,10 @@ def tile_moe_sup_lin_gelu_kernel(
         for e in range(2):
             nc.sync.dma_start(w2_first[e][:], w2[e].rearrange("(p j) n -> p j n", j=4))
         nc.sync.dma_start(offs_sb[:], offs)
-        w2_raw = {g: held([P, 2, 4, N], F32, "w2_raw%d" % g, "w2_raw%d" % g) for g in range(2, PAIRS)}
-        w2_raw[1] = placed([P, 2, 4, N], F32, "w2_raw1", 0)
-        for g in range(1, PAIRS):
-            nc.sync.dma_start(w2_raw[g][:], w2[2 * g : 2 * g + 2].rearrange("e (p j) n -> p e j n", j=4))
+        w2_raw = {e: held([P, 4, N], F32, "w2_raw%d" % e, "w2_raw%d" % e) for e in range(2, E) if e != 4}
+        w2_raw[4] = placed([P, 4, N], F32, "w2_raw4", 0)
+        for e in range(2, E):
+            nc.sync.dma_start(w2_raw[e][:], w2[e].rearrange("(p j) n -> p j n", j=4))
         for r, pos in enumerate((pos1, pos2, pos3, pos4)):
             nc.sync.dma_start(pos_sb[r][:], pos)
         gate_sb = held([P, TOP, T], F32, "gate_sb")
@@ -161,24 +160,23 @@ def tile_moe_sup_lin_gelu_kernel(
                 )
             nc.scalar.copy(y[half][:, 2 * g * C : (2 * g + 2) * C], bank[:])
 
-        def cast_gpsimd(g, half, dst):
+        w2_cast = held([P, 2, (E - 2) * P, 4], BF16, "w2_cast")
+
+        def cast_gpsimd(e):
             nc.gpsimd.tensor_scalar(
-                dst.rearrange("p (e n) j -> p e n j", e=2),
-                w2_raw[g][:, :, :, half * P : (half + 1) * P].rearrange("p e j n -> p e n j"),
+                w2_cast[:, :, (e - 2) * P : (e - 1) * P, :],
+                w2_raw[e][:].rearrange("p j (h n) -> p h n j", h=2),
                 1.0, 0.0, MULT, ADD,
             )
 
-        def cast_runs(src, dst, copy):
-            copy(
-                dst.rearrange("p (e c i) j -> p e c j i", e=2, i=4),
-                src.rearrange("p e j (c i) -> p e c j i", i=4),
+        def cast_scalar(e):
+            nc.scalar.copy(
+                w2_cast[:, :, (e - 2) * P : (e - 1) * P, :].rearrange("p h (c i) j -> p h c j i", i=4),
+                w2_raw[e][:].rearrange("p j (h c i) -> p h c j i", h=2, i=4),
             )
 
-        def cast_scalar(g, dst):
-            cast_runs(w2_raw[g][:, :, :, P:N], dst, nc.scalar.copy)
-
-        def quantize_w(src, pairs, half, offset=None):
-            quantize(src, [(("w", 2 * g + a, half), P) for g in pairs for a in range(2)], offset)
+        def quantize_w(e0, e1, half, offset=None):
+            quantize(w2_cast[:, half, (e0 - 2) * P : (e1 - 2) * P, :], [(("w", e, half), P) for e in range(e0, e1)], offset)
 
         def cast_first(e, n0, n1, dst, copy):
             copy(
@@ -193,59 +191,56 @@ def tile_moe_sup_lin_gelu_kernel(
         cast_first(1, 0, P, first_b[:], nc.vector.tensor_copy)
         quantize(first_b[:], [(("w", 1, 0), P)])
         late_first = held([P, P, 4], BF16, "late_first", "x_sb")
+        for e in range(3, E, 2):
+            cast_gpsimd(e)
+        cast_scalar(2)
         cast_first(1, P, N, late_first[:], nc.scalar.copy)
+        cast_scalar(4)
 
-        early_14 = held([P, 4 * C, 4], BF16, "early_14")
-        early_5 = held([P, C, 4], BF16, "early_5")
-        late_14 = held([P, 4 * C, 4], BF16, "late_14")
-        late_5 = held([P, C, 4], BF16, "late_5")
-        for g in range(1, 5):
-            cast_gpsimd(g, 0, early_14[:, (g - 1) * C : g * C, :])
-        cast_gpsimd(5, 0, early_5[:])
-        cast_gpsimd(5, 1, late_5[:])
-        for g in range(1, 5):
-            cast_scalar(g, late_14[:, (g - 1) * C : g * C, :])
-
-        picked = [held([P, 2, S // 2], U32, "picked0", "picked0"), placed([P, 2, S // 2], U32, "picked1", 0)]
+        picked = [
+            held([P, 2, 4 * C], U32, "picked0", "picked0"),
+            held([P, 2, 4 * C], U32, "picked1", "w2_raw2"),
+            placed([P, 2, 4 * C], U32, "picked2", 0),
+        ]
+        staged = {g0: held([P, (g1 - g0) * 2 * C, 4], BF16, "staged%d" % g0) for g0, g1 in GATHERS}
         for g0, g1 in GATHERS:
             for u in range(2):
                 nc.vector.tensor_copy(
-                    picked[g0 // 3][:, u, g0 % 3 * 2 * C : (g0 % 3 + g1 - g0) * 2 * C],
+                    picked[g0 // 2][:, u, g0 % 2 * 2 * C : (g0 % 2 + g1 - g0) * 2 * C],
                     h_pairs[u][:].indirect(offs_sb[:, g0 * 2 * C // 16 : g1 * 2 * C // 16]),
                 )
-        staged = {}
-        for (g0, g1), tag in zip(UNITS, ("w2_raw3", "w2_raw4", "picked0", "w2_raw5")):
-            tile = held([P, (g1 - g0) * 2 * C, 4], BF16, "staged%d" % g0, tag)
-            for g in range(g0, g1):
-                staged[g] = (tile, g0)
 
         def interleave_h(g0, g1):
-            dst, d0 = staged[g0]
             nc.scalar.copy(
-                dst[:, (g0 - d0) * 2 * C : (g1 - d0) * 2 * C, :].rearrange("p s j -> p (s j)").bitcast(F32).rearrange("p (s u) -> p s u", u=2),
-                picked[g0 // 3][:, :, g0 % 3 * 2 * C : (g0 % 3 + g1 - g0) * 2 * C].bitcast(F32).rearrange("p u s -> p s u"),
+                staged[g0][:].rearrange("p s j -> p (s j)").bitcast(F32).rearrange("p (s u) -> p s u", u=2),
+                picked[g0 // 2][:, :, g0 % 2 * 2 * C : (g0 % 2 + g1 - g0) * 2 * C].bitcast(F32).rearrange("p u s -> p s u"),
             )
 
-        for g0, g1 in ((0, 2), (2, 3), (3, 4), (4, 5), (5, 6)):
-            interleave_h(g0, g1)
+        interleave_h(0, 2)
+        cast_scalar(6)
+        cast_scalar(8)
+        interleave_h(2, 4)
+        cast_scalar(10)
+        interleave_h(4, 5)
+        interleave_h(5, 6)
 
         def quantize_h(g0, g1):
-            quantize(staged[g0][0][:], [(("h", e), C) for e in range(2 * g0, 2 * g1)])
+            quantize(staged[g0][:], [(("h", e), C) for e in range(2 * g0, 2 * g1)])
 
         quantize_h(0, 2)
         second_layer(0, 0, banks[0])
-        quantize_w(early_14[:], (1, 2, 3, 4), 0)
+        quantize_w(2, 10, 0)
         second_layer(1, 0, banks[1])
-        quantize_w(early_5[:], (5,), 0)
         quantize_h(2, 4)
         second_layer(2, 0, banks[2])
         second_layer(3, 0, banks[3])
+        quantize_w(10, E, 0)
         quantize_h(4, 5)
         second_layer(4, 0, banks[4])
         quantize_h(5, 6)
         second_layer(5, 0, banks[5])
-        quantize_w(late_14[:], (1, 2, 3, 4), 1, 0)
-        quantize_w(late_5[:], (5,), 1, 1024)
+        quantize_w(2, 10, 1, 0)
+        quantize_w(10, E, 1, 1024)
         quantize(late_first[:], [(("w", 1, 1), P)], 1280)
         for g in (1, 2, 3, 4, 5, 0):
             second_layer(g, 1, banks[2 + (g + 3) % 6])
@@ -272,7 +267,7 @@ def tile_moe_sup_lin_gelu_kernel(
                 nc.tensor.transpose(back[:, b * P : (b + 1) * P], turned[:, b * P : (b + 1) * P], ident[:])
 
         terms = held([P, TOP, T], F32, "terms_first", "picked0")
-        result = held([P, T], F32, "result_first", "w2_raw5")
+        result = held([P, T], F32, "result_first", "w2_raw3")
         for r in range(TOP):
             gather_term(terms[:, r, :], r, 0, 0, T)
             add_turned(banks[0], terms[:, r, :], 0, 3, r == 0, r == TOP - 1)
@@ -283,7 +278,7 @@ def tile_moe_sup_lin_gelu_kernel(
             nc.scalar.copy(result[:, 3 * k * P : (3 * k + 3) * P], banks[2 + k][:, 0 : 3 * P])
         nc.scalar.dma_start(out[0:P, :], result[:])
 
-        terms = held([P, TOP, T], F32, "terms_second", "w2_raw3")
+        terms = held([P, TOP, T], F32, "terms_second", "w2_raw2")
         for r in range(2):
             gather_term(terms[:, r, :], r, 1, 0, T)
             for k in range(3):

@@ -23,7 +23,7 @@ PASSES = K // 512
 CHUNKS = ((0, 256), (256, 256), (512, 128), (640, 128))
 PAIRS = E // 2
 WINDOW = 1536
-GATHERS = ((0, 2), (2, 4), (4, 5), (5, 6))
+GATHERS = ((0, 2), (2, 4), (4, 6))
 
 
 def tile_moe_sup_lin_gelu_kernel(
@@ -49,7 +49,7 @@ def tile_moe_sup_lin_gelu_kernel(
 
         w1_raw = held([P, PASSES, H], U32, "w1_raw")
         w1s_raw = held([P, PASSES, H], U8, "w1s_raw")
-        x_sb = held([P, PASSES, T], U32, "x_sb", "x_sb")
+        x_sb = held([P, PASSES, T], U32, "x_sb")
         xs_sb = held([P, PASSES, T], U8, "xs_sb")
         nc.vector.memset(w1s_raw[:].rearrange("p s n -> p (s n)").bitcast(I32), 0)
         nc.vector.memset(xs_sb[:].rearrange("p s n -> p (s n)").bitcast(I32), 0)
@@ -65,14 +65,12 @@ def tile_moe_sup_lin_gelu_kernel(
             if r == 2:
                 nc.sync.dma_start(x_sb[:].bitcast(I32), x_words.rearrange("s p t d -> p s (t d)").bitcast(I32))
             load_scales(xs_sb, 4, x_scales, r)
-        w2_first = [held([P, 4, N], F32, "w2_first%d" % e) for e in range(2)]
-        for e in range(2):
-            nc.sync.dma_start(w2_first[e][:], w2[e].rearrange("(p j) n -> p j n", j=4))
-        nc.sync.dma_start(offs_sb[:], offs)
-        w2_raw = {e: held([P, 4, N], F32, "w2_raw%d" % e, "w2_raw%d" % e) for e in range(2, E) if e != 4}
+        w2_raw = {e: held([P, 4, N], F32, "w2_raw%d" % e, "w2_raw%d" % e) for e in range(E) if e != 4}
         w2_raw[4] = placed([P, 4, N], F32, "w2_raw4", 0)
-        for e in range(2, E):
+        for e in range(E):
             nc.sync.dma_start(w2_raw[e][:], w2[e].rearrange("(p j) n -> p j n", j=4))
+            if e == 0:
+                nc.sync.dma_start(offs_sb[:], offs)
         for r, pos in enumerate((pos1, pos2, pos3, pos4)):
             nc.sync.dma_start(pos_sb[r][:], pos)
         gate_sb = held([P, TOP, T], F32, "gate_sb")
@@ -164,45 +162,49 @@ def tile_moe_sup_lin_gelu_kernel(
 
         def cast_gpsimd(e):
             nc.gpsimd.tensor_scalar(
-                w2_cast[:, :, (e - 2) * P : (e - 1) * P, :],
+                w2_cast[:, :, (e - 1) * P : e * P, :],
                 w2_raw[e][:].rearrange("p j (h n) -> p h n j", h=2),
                 1.0, 0.0, MULT, ADD,
             )
 
         def cast_scalar(e):
             nc.scalar.copy(
-                w2_cast[:, :, (e - 2) * P : (e - 1) * P, :].rearrange("p h (c i) j -> p h c j i", i=4),
+                w2_cast[:, :, (e - 1) * P : e * P, :].rearrange("p h (c i) j -> p h c j i", i=4),
                 w2_raw[e][:].rearrange("p j (h c i) -> p h c j i", h=2, i=4),
             )
 
         def quantize_w(e0, e1, half, offset=None):
-            quantize(w2_cast[:, half, (e0 - 2) * P : (e1 - 2) * P, :], [(("w", e, half), P) for e in range(e0, e1)], offset)
+            quantize(w2_cast[:, half, (e0 - 1) * P : (e1 - 1) * P, :], [(("w", e, half), P) for e in range(e0, e1)], offset)
 
-        def cast_first(e, n0, n1, dst, copy):
+        whole = {e: held([P, N, 4], BF16, "whole%d" % e) for e in (0, E - 1)}
+
+        def cast_whole(e, copy):
             copy(
-                dst.rearrange("p (c i) j -> p c j i", i=4),
-                w2_first[e][:, :, n0:n1].rearrange("p j (c i) -> p c j i", i=4),
+                whole[e][:].rearrange("p (c i) j -> p c j i", i=4),
+                w2_raw[e][:].rearrange("p j (c i) -> p c j i", i=4),
             )
 
-        first_a = held([P, N, 4], BF16, "first_a")
-        first_b = held([P, P, 4], BF16, "first_b")
-        cast_first(0, 0, N, first_a[:], nc.vector.tensor_copy)
-        quantize(first_a[:], [(("w", 0, 0), P), (("w", 0, 1), P)])
-        cast_first(1, 0, P, first_b[:], nc.vector.tensor_copy)
-        quantize(first_b[:], [(("w", 1, 0), P)])
-        late_first = held([P, P, 4], BF16, "late_first", "x_sb")
-        for e in range(3, E, 2):
+        def quantize_whole(e):
+            quantize(whole[e][:], [(("w", e, 0), P), (("w", e, 1), P)])
+
+        cast_whole(0, nc.vector.tensor_copy)
+        quantize_whole(0)
+        for e in (1, 3, 4, 5, 7, 8, 9):
             cast_gpsimd(e)
         cast_scalar(2)
-        cast_first(1, P, N, late_first[:], nc.scalar.copy)
-        cast_scalar(4)
 
         picked = [
             held([P, 2, 4 * C], U32, "picked0", "picked0"),
             held([P, 2, 4 * C], U32, "picked1", "w2_raw2"),
             placed([P, 2, 4 * C], U32, "picked2", 0),
         ]
-        staged = {g0: held([P, (g1 - g0) * 2 * C, 4], BF16, "staged%d" % g0) for g0, g1 in GATHERS}
+        staged = [
+            held([P, 4 * C, 4], BF16, "staged%d" % k, tag) for k, tag in enumerate(("staged0", "w2_raw6", "w2_raw11"))
+        ]
+
+        def slots(g0, g1):
+            return slice(g0 % 2 * 2 * C, (g0 % 2 + g1 - g0) * 2 * C)
+
         for g0, g1 in GATHERS:
             for u in range(2):
                 nc.vector.tensor_copy(
@@ -212,38 +214,39 @@ def tile_moe_sup_lin_gelu_kernel(
 
         def interleave_h(g0, g1):
             nc.scalar.copy(
-                staged[g0][:].rearrange("p s j -> p (s j)").bitcast(F32).rearrange("p (s u) -> p s u", u=2),
-                picked[g0 // 2][:, :, g0 % 2 * 2 * C : (g0 % 2 + g1 - g0) * 2 * C].bitcast(F32).rearrange("p u s -> p s u"),
+                staged[g0 // 2][:, slots(g0, g1), :].rearrange("p s j -> p (s j)").bitcast(F32).rearrange("p (s u) -> p s u", u=2),
+                picked[g0 // 2][:, :, slots(g0, g1)].bitcast(F32).rearrange("p u s -> p s u"),
             )
 
         interleave_h(0, 2)
         cast_scalar(6)
-        cast_scalar(8)
         interleave_h(2, 4)
         cast_scalar(10)
+        cast_whole(E - 1, nc.scalar.copy)
         interleave_h(4, 5)
         interleave_h(5, 6)
 
         def quantize_h(g0, g1):
-            quantize(staged[g0][:], [(("h", e), C) for e in range(2 * g0, 2 * g1)])
+            quantize(staged[g0 // 2][:, slots(g0, g1), :], [(("h", e), C) for e in range(2 * g0, 2 * g1)])
 
+        quantize_w(1, 5, 0)
         quantize_h(0, 2)
         second_layer(0, 0, banks[0])
-        quantize_w(2, 10, 0)
         second_layer(1, 0, banks[1])
+        quantize_w(5, 9, 0)
         quantize_h(2, 4)
         second_layer(2, 0, banks[2])
         second_layer(3, 0, banks[3])
-        quantize_w(10, E, 0)
+        quantize_w(9, 11, 0)
         quantize_h(4, 5)
         second_layer(4, 0, banks[4])
+        quantize_whole(E - 1)
         quantize_h(5, 6)
         second_layer(5, 0, banks[5])
-        quantize_w(2, 10, 1, 0)
-        quantize_w(10, E, 1, 1024)
-        quantize(late_first[:], [(("w", 1, 1), P)], 1280)
-        for g in (1, 2, 3, 4, 5, 0):
-            second_layer(g, 1, banks[2 + (g + 3) % 6])
+        quantize_w(1, 9, 1, 0)
+        quantize_w(9, 11, 1, 1024)
+        for g in range(PAIRS):
+            second_layer(g, 1, banks[2 + (g + 4) % 6])
 
         def gather_term(term, r, half, t0, width):
             nc.vector.tensor_tensor(

@@ -23,7 +23,7 @@ PASSES = K // 512
 CHUNKS = ((0, 256), (256, 256), (512, 128), (640, 128))
 PAIRS = E // 2
 WINDOW = 1536
-GATHERS = ((0, 2), (2, 4), (4, 6))
+GATHERS = ((0, 0, 2), (1, 0, 2), (0, 2, 4), (1, 2, 4), (0, 4, 6), (1, 4, 5), (1, 5, 6))
 
 
 def tile_moe_sup_lin_gelu_kernel(
@@ -143,10 +143,10 @@ def tile_moe_sup_lin_gelu_kernel(
                 quantized[name] = (codes[:, col : col + width], scales[:, col : col + width])
                 col = col + width
 
-        def second_layer(g, half, bank):
-            for a in range(2):
-                w_codes, w_scales = quantized["w", 2 * g + a, half]
-                h_codes, h_scales = quantized["h", 2 * g + a]
+        def second_layer(experts, half, bank):
+            for a, e in enumerate(experts):
+                w_codes, w_scales = quantized["w", e, half]
+                h_codes, h_scales = quantized["h", e]
                 nc.tensor.matmul_mx(
                     out=bank[:, a * C : (a + 1) * C],
                     lhsT=w_codes.bitcast(FP8X4),
@@ -156,9 +156,8 @@ def tile_moe_sup_lin_gelu_kernel(
                     start=True,
                     stop=True,
                 )
-            nc.scalar.copy(y[half][:, 2 * g * C : (2 * g + 2) * C], bank[:])
+            nc.scalar.copy(y[half][:, experts[0] * C : (experts[-1] + 1) * C], bank[:, 0 : len(experts) * C])
 
-        w2_cast = held([P, 2, (E - 2) * P, 4], BF16, "w2_cast")
 
         def cast_gpsimd(e):
             nc.gpsimd.tensor_scalar(
@@ -176,22 +175,17 @@ def tile_moe_sup_lin_gelu_kernel(
         def quantize_w(e0, e1, half, offset=None):
             quantize(w2_cast[:, half, (e0 - 1) * P : (e1 - 1) * P, :], [(("w", e, half), P) for e in range(e0, e1)], offset)
 
-        whole = {e: held([P, N, 4], BF16, "whole%d" % e) for e in (0, E - 1)}
-
-        def cast_whole(e, copy):
-            copy(
-                whole[e][:].rearrange("p (c i) j -> p c j i", i=4),
-                w2_raw[e][:].rearrange("p j (c i) -> p c j i", i=4),
-            )
-
-        def quantize_whole(e):
-            quantize(whole[e][:], [(("w", e, 0), P), (("w", e, 1), P)])
-
-        cast_whole(0, nc.vector.tensor_copy)
-        quantize_whole(0)
-        for e in (1, 3, 4, 5, 7, 8, 9):
+        first_cast = held([P, N, 4], BF16, "first_cast", "w2_cast")
+        nc.vector.tensor_copy(
+            first_cast[:].rearrange("p (c i) j -> p c j i", i=4),
+            w2_raw[0][:].rearrange("p j (c i) -> p c j i", i=4),
+        )
+        quantize(first_cast[:], [(("w", 0, 0), P), (("w", 0, 1), P)])
+        w2_cast = held([P, 2, (E - 1) * P, 4], BF16, "w2_cast", "w2_cast")
+        for e in (1, 4, 5, 7, 8, 9, 10):
             cast_gpsimd(e)
         cast_scalar(2)
+        cast_scalar(3)
 
         picked = [
             held([P, 2, 4 * C], U32, "picked0", "picked0"),
@@ -205,12 +199,10 @@ def tile_moe_sup_lin_gelu_kernel(
         def slots(g0, g1):
             return slice(g0 % 2 * 2 * C, (g0 % 2 + g1 - g0) * 2 * C)
 
-        for g0, g1 in GATHERS:
-            for u in range(2):
-                nc.vector.tensor_copy(
-                    picked[g0 // 2][:, u, g0 % 2 * 2 * C : (g0 % 2 + g1 - g0) * 2 * C],
-                    h_pairs[u][:].indirect(offs_sb[:, g0 * 2 * C // 16 : g1 * 2 * C // 16]),
-                )
+        for u, g0, g1 in GATHERS:
+            nc.vector.tensor_copy(
+                picked[g0 // 2][:, u, slots(g0, g1)], h_pairs[u][:].indirect(offs_sb[:, g0 * 2 * C // 16 : g1 * 2 * C // 16])
+            )
 
         def interleave_h(g0, g1):
             nc.scalar.copy(
@@ -221,32 +213,34 @@ def tile_moe_sup_lin_gelu_kernel(
         interleave_h(0, 2)
         cast_scalar(6)
         interleave_h(2, 4)
-        cast_scalar(10)
-        cast_whole(E - 1, nc.scalar.copy)
+        cast_scalar(11)
         interleave_h(4, 5)
         interleave_h(5, 6)
 
-        def quantize_h(g0, g1):
-            quantize(staged[g0 // 2][:, slots(g0, g1), :], [(("h", e), C) for e in range(2 * g0, 2 * g1)])
+        def quantize_h(e0, e1):
+            quantize(staged[e0 // 4][:, e0 % 4 * C : (e0 % 4 + e1 - e0) * C, :], [(("h", e), C) for e in range(e0, e1)])
 
         quantize_w(1, 5, 0)
-        quantize_h(0, 2)
-        second_layer(0, 0, banks[0])
-        second_layer(1, 0, banks[1])
+        quantize_h(0, 4)
+        second_layer((0, 1), 0, banks[0])
+        second_layer((2, 3), 0, banks[1])
         quantize_w(5, 9, 0)
-        quantize_h(2, 4)
-        second_layer(2, 0, banks[2])
-        second_layer(3, 0, banks[3])
+        quantize_h(4, 6)
+        second_layer((4, 5), 0, banks[2])
+        quantize_h(6, 8)
+        second_layer((6, 7), 0, banks[3])
         quantize_w(9, 11, 0)
-        quantize_h(4, 5)
-        second_layer(4, 0, banks[4])
-        quantize_whole(E - 1)
-        quantize_h(5, 6)
-        second_layer(5, 0, banks[5])
+        quantize_h(8, 10)
+        second_layer((8, 9), 0, banks[4])
+        quantize_w(11, E, 0)
+        for e in (10, 11):
+            quantize_h(e, e + 1)
+            second_layer((e,), 0, banks[e - 5])
         quantize_w(1, 9, 1, 0)
         quantize_w(9, 11, 1, 1024)
+        quantize_w(11, E, 1, 1280)
         for g in range(PAIRS):
-            second_layer(g, 1, banks[2 + (g + 4) % 6])
+            second_layer((2 * g, 2 * g + 1), 1, banks[2 + (g + 5) % 6])
 
         def gather_term(term, r, half, t0, width):
             nc.vector.tensor_tensor(

@@ -23,6 +23,10 @@ PASSES = K // 512
 CHUNKS = ((0, 256), (256, 256), (512, 128), (640, 128))
 PAIRS = E // 2
 WINDOW = 1536
+EARLY = 5
+FRONT = 384
+BLOCKS = (T - FRONT) // P
+COPY = mybir.ActivationFunctionType.Copy
 GATHERS = ((0, 0, 2), (1, 0, 2), (0, 2, 4), (1, 2, 4), (0, 4, 6), (1, 4, 5), (1, 5, 6))
 
 
@@ -66,15 +70,21 @@ def tile_moe_sup_lin_gelu_kernel(
                 nc.sync.dma_start(x_sb[:].bitcast(I32), x_words.rearrange("s p t d -> p s (t d)").bitcast(I32))
             load_scales(xs_sb, 4, x_scales, r)
         w2_raw = {e: held([P, 4, N], F32, "w2_raw%d" % e, "w2_raw%d" % e) for e in range(E) if e != 4}
-        w2_raw[4] = placed([P, 4, N], F32, "w2_raw4", 0)
+        w2_raw[4] = placed([P, 4, N], F32, "w2_raw4", 8192)
         for e in range(E):
             nc.sync.dma_start(w2_raw[e][:], w2[e].rearrange("(p j) n -> p j n", j=4))
             if e == 0:
                 nc.sync.dma_start(offs_sb[:], offs)
         for r, pos in enumerate((pos1, pos2, pos3, pos4)):
             nc.sync.dma_start(pos_sb[r][:], pos)
-        gate_sb = held([P, TOP, T], F32, "gate_sb")
-        nc.sync.dma_start(gate_sb[:], gate.rearrange("r p t -> p r t"))
+        gate_front = held([P, TOP - 1, FRONT], F32, "gate_front")
+        nc.sync.dma_start(gate_front[:], gate[0 : TOP - 1, :, 0:FRONT].rearrange("r p t -> p r t"))
+        gate_last = held([P, T], F32, "gate_last")
+        nc.sync.dma_start(gate_last[:], gate[TOP - 1])
+        gate_turned = held([P, TOP - 1, 8], F32, "gate_turned")
+        with nc.allow_non_contiguous_dma(reason="one gate value a token, a token a partition"):
+            for r in range(TOP - 1):
+                nc.sync.dma_start(gate_turned[:, r, 0:BLOCKS], gate[r, 0, FRONT:T].rearrange("(b p) -> p b", p=P))
 
         ident = held([P, P], F32, "ident")
         make_identity(nc, ident[:])
@@ -102,7 +112,7 @@ def tile_moe_sup_lin_gelu_kernel(
                 stop=True,
             )
 
-        h_pairs = [held([P, WINDOW], U32, "h_pairs%d" % u) for u in range(2)]
+        h_pairs = [held([P, WINDOW], U32, "h_pairs%d" % u, "h_pairs%d" % u) for u in range(2)]
         for u in range(2):
             nc.vector.memset(h_pairs[u][:, T:WINDOW], 0)
         for u in range(2):
@@ -126,13 +136,13 @@ def tile_moe_sup_lin_gelu_kernel(
                     GELU,
                 )
 
-        y = [placed([P, S], F32, "y0", 2048), held([P, S], F32, "y1")]
+        y = [placed([P, S], F32, "y0", 14336), placed([P, S], F32, "y1", 0)]
         quantized = {}
 
-        def quantize(src, names, offset=None):
+        def quantize(src, names, offset=None, tag=""):
             words = sum(width for name, width in names)
             label = "_".join(str(part) for part in names[0][0])
-            codes = held([P, words], U32, "codes_" + label)[:]
+            codes = held([P, words], U32, "codes_" + label, tag)[:]
             if offset is None:
                 scales = held([P, words], U8, "scales_" + label)
             else:
@@ -159,21 +169,26 @@ def tile_moe_sup_lin_gelu_kernel(
             nc.scalar.copy(y[half][:, experts[0] * C : (experts[-1] + 1) * C], bank[:, 0 : len(experts) * C])
 
 
+        def cast_view(e):
+            if e < EARLY:
+                return early_cast[:, e - 1, :, :].rearrange("p (h n) j -> p h n j", h=2)
+            return late_cast[:, :, (e - EARLY) * P : (e - EARLY + 1) * P, :]
+
         def cast_gpsimd(e):
             nc.gpsimd.tensor_scalar(
-                w2_cast[:, :, (e - 1) * P : e * P, :],
+                cast_view(e),
                 w2_raw[e][:].rearrange("p j (h n) -> p h n j", h=2),
                 1.0, 0.0, MULT, ADD,
             )
 
         def cast_scalar(e):
             nc.scalar.copy(
-                w2_cast[:, :, (e - 1) * P : e * P, :].rearrange("p h (c i) j -> p h c j i", i=4),
+                cast_view(e).rearrange("p h (c i) j -> p h c j i", i=4),
                 w2_raw[e][:].rearrange("p j (h c i) -> p h c j i", h=2, i=4),
             )
 
         def quantize_w(e0, e1, half, offset=None):
-            quantize(w2_cast[:, half, (e0 - 1) * P : (e1 - 1) * P, :], [(("w", e, half), P) for e in range(e0, e1)], offset)
+            quantize(late_cast[:, half, (e0 - EARLY) * P : (e1 - EARLY) * P, :], [(("w", e, half), P) for e in range(e0, e1)], offset)
 
         first_cast = held([P, N, 4], BF16, "first_cast", "w2_cast")
         nc.vector.tensor_copy(
@@ -181,7 +196,8 @@ def tile_moe_sup_lin_gelu_kernel(
             w2_raw[0][:].rearrange("p j (c i) -> p c j i", i=4),
         )
         quantize(first_cast[:], [(("w", 0, 0), P), (("w", 0, 1), P)])
-        w2_cast = held([P, 2, (E - 1) * P, 4], BF16, "w2_cast", "w2_cast")
+        early_cast = held([P, EARLY - 1, N, 4], BF16, "early_cast", "w2_cast")
+        late_cast = held([P, 2, (E - EARLY) * P, 4], BF16, "late_cast")
         for e in (1, 4, 5, 7, 8, 9, 10):
             cast_gpsimd(e)
         cast_scalar(2)
@@ -190,7 +206,7 @@ def tile_moe_sup_lin_gelu_kernel(
         picked = [
             held([P, 2, 4 * C], U32, "picked0", "picked0"),
             held([P, 2, 4 * C], U32, "picked1", "w2_raw2"),
-            placed([P, 2, 4 * C], U32, "picked2", 0),
+            placed([P, 2, 4 * C], U32, "picked2", 8192),
         ]
         staged = [
             held([P, 4 * C, 4], BF16, "staged%d" % k, tag) for k, tag in enumerate(("staged0", "w2_raw6", "w2_raw11"))
@@ -220,78 +236,111 @@ def tile_moe_sup_lin_gelu_kernel(
         def quantize_h(e0, e1):
             quantize(staged[e0 // 4][:, e0 % 4 * C : (e0 % 4 + e1 - e0) * C, :], [(("h", e), C) for e in range(e0, e1)])
 
-        quantize_w(1, 5, 0)
-        quantize_h(0, 4)
+        def quantize_early(e0, e1, tag=""):
+            names = [(("w", e, half), P) for e in range(e0, e1) for half in range(2)]
+            quantize(early_cast[:, e0 - 1 : e1 - 1, :, :].rearrange("p e n j -> p (e n) j"), names, None, tag)
+
+        quantize_early(1, 3, "h_pairs0")
+        quantize_h(0, 2)
         second_layer((0, 1), 0, banks[0])
+        second_layer((0, 1), 1, banks[6])
+        quantize_h(2, 4)
+        quantize_early(3, EARLY)
         second_layer((2, 3), 0, banks[1])
+        second_layer((2, 3), 1, banks[7])
         quantize_w(5, 9, 0)
         quantize_h(4, 6)
         second_layer((4, 5), 0, banks[2])
         quantize_h(6, 8)
         second_layer((6, 7), 0, banks[3])
-        quantize_w(9, 11, 0)
+        quantize_w(9, E, 0)
         quantize_h(8, 10)
         second_layer((8, 9), 0, banks[4])
-        quantize_w(11, E, 0)
-        for e in (10, 11):
-            quantize_h(e, e + 1)
-            second_layer((e,), 0, banks[e - 5])
-        quantize_w(1, 9, 1, 0)
-        quantize_w(9, 11, 1, 1024)
-        quantize_w(11, E, 1, 1280)
-        for g in range(PAIRS):
-            second_layer((2 * g, 2 * g + 1), 1, banks[2 + (g + 5) % 6])
+        quantize_h(10, 11)
+        second_layer((10,), 0, banks[5])
+        quantize_h(11, E)
+        second_layer((11,), 0, banks[0])
+        quantize_w(5, 9, 1, 12288)
+        quantize_w(9, E, 1, 12800)
+        for g in range(2, PAIRS):
+            second_layer((2 * g, 2 * g + 1), 1, banks[g - 1])
 
-        def gather_term(term, r, half, t0, width):
-            nc.vector.tensor_tensor(
-                term[:, t0 : t0 + width],
-                y[half][:].indirect(pos_sb[r][:, t0 // 16 : (t0 + width) // 16]),
-                gate_sb[:, r, t0 : t0 + width],
-                MULT,
-            )
+        def offsets(r, t0, width):
+            return pos_sb[r][:, t0 // 16 : (t0 + width) // 16]
 
-        def add_turned(bank, term, b0, b1, first, last):
-            for b in range(b0, b1):
-                nc.tensor.matmul(
-                    bank[:, (b - b0) * P : (b - b0 + 1) * P], lhsT=term[:, b * P : (b + 1) * P], rhs=ident[:],
-                    start=(first and b == b0), stop=(last and b == b1 - 1), is_transpose=True,
-                )
+        def turn(dst, src, first, last):
+            nc.tensor.matmul(dst, lhsT=src, rhs=ident[:], start=first, stop=last, is_transpose=True)
 
-        def turn_back(total, back, b0, b1, name):
-            turned = held([P, (b1 - b0) * P], F32, "turned" + name)
-            nc.scalar.copy(turned[:], total[:, 0 : (b1 - b0) * P])
-            for b in range(b1 - b0):
-                nc.tensor.transpose(back[:, b * P : (b + 1) * P], turned[:, b * P : (b + 1) * P], ident[:])
+        front_terms = [held([P, TOP - 1, FRONT], F32, "front_terms%d" % half, ("picked0", "w2_raw2")[half]) for half in range(2)]
+        front_sums = [held([P, 2, FRONT], F32, "front_sums%d" % half, "w2_raw%d" % (1 + 2 * half)) for half in range(2)]
+        last_term = held([P, 2, T], F32, "last_term", "staged0")
+        back_terms = {(r, half): held([P, T - FRONT], F32, "back_terms%d%d" % (r, half)) for r in range(TOP - 1) for half in range(2)}
+        gated = {(r, b): held([P, N], F32, "gated%d%d" % (r, b))[:] for r in range(1, TOP - 1) for b in range(BLOCKS)}
+        for b, later in enumerate(((1, 1), (2, 0), (2, 1))):
+            gated[0, b] = back_terms[later][:, 0:N]
+        back_banks = (banks[3], banks[4], banks[2])
 
-        terms = held([P, TOP, T], F32, "terms_first", "picked0")
-        result = held([P, T], F32, "result_first", "w2_raw3")
-        for r in range(TOP):
-            gather_term(terms[:, r, :], r, 0, 0, T)
-            add_turned(banks[0], terms[:, r, :], 0, 3, r == 0, r == TOP - 1)
-            add_turned(banks[1], terms[:, r, :], 3, 6, r == 0, r == TOP - 1)
-        for k in range(2):
-            turn_back(banks[k], banks[2 + k], 3 * k, 3 * k + 3, "first%d" % k)
-        for k in range(2):
-            nc.scalar.copy(result[:, 3 * k * P : (3 * k + 3) * P], banks[2 + k][:, 0 : 3 * P])
-        nc.scalar.dma_start(out[0:P, :], result[:])
+        def turned_sums(r, b):
+            if b < 2:
+                return banks[(7, 0, 1)[r]][:, b * N : (b + 1) * N]
+            return banks[(6, 5, 7)[r]][:, 0:N]
 
-        terms = held([P, TOP, T], F32, "terms_second", "w2_raw2")
-        for r in range(2):
-            gather_term(terms[:, r, :], r, 1, 0, T)
-            for k in range(3):
-                add_turned(banks[4 + k], terms[:, r, :], 2 * k, 2 * k + 2, r == 0, False)
-        gather_term(terms[:, 2, :], 2, 1, 0, C)
-        gather_term(terms[:, 2, :], 2, 1, C, 2 * C)
-        backs = (banks[7], banks[0], banks[1])
-        add_turned(banks[4], terms[:, 2, :], 0, 2, False, True)
-        turn_back(banks[4], backs[0], 0, 2, "second0")
-        for k in range(1, 3):
-            add_turned(banks[4 + k], terms[:, 2, :], 2 * k, 2 * k + 2, False, True)
-        for k in range(1, 3):
-            turn_back(banks[4 + k], backs[k], 2 * k, 2 * k + 2, "second%d" % k)
-        for k in range(3):
-            gather_term(terms[:, 3, :], 3, 1, k * C, C)
-        for k in range(3):
-            result = held([P, C], F32, "result_second%d" % k)
-            nc.vector.tensor_tensor(result[:], terms[:, 3, k * C : (k + 1) * C], backs[k][:, 0:C], ADD)
-            nc.sync.dma_start(out[P:N, k * C : (k + 1) * C], result[:])
+        def front_gather(half, r):
+            nc.vector.tensor_tensor(front_terms[half][:, r, :], y[half][:].indirect(offsets(r, 0, FRONT)), gate_front[:, r, :], MULT)
+
+        def front_add(half, k):
+            first = front_terms[half][:, 0, :] if k == 0 else front_sums[half][:, 0, :]
+            nc.vector.tensor_tensor(front_sums[half][:, k, :], first, front_terms[half][:, k + 1, :], ADD)
+
+        def front_finish(half):
+            result = held([P, FRONT], F32, "front_result%d" % half, "w2_raw%d" % (5 * half))
+            nc.vector.tensor_tensor(result[:], last_term[:, half, 0:FRONT], front_sums[half][:, 1, :], ADD)
+            nc.sync.dma_start(out[half * P : (half + 1) * P, 0:FRONT], result[:])
+
+        def last_gather(half):
+            nc.vector.tensor_tensor(last_term[:, half, :], y[half][:].indirect(pos_sb[TOP - 1][:]), gate_last[:], MULT)
+
+        def back_gather(r, half):
+            term = back_terms[r, half][:]
+            nc.scalar.activation(term, y[half][:].indirect(offsets(r, FRONT, T - FRONT)), COPY)
+            for b in range(BLOCKS):
+                turn(turned_sums(r, b)[:, half * P : (half + 1) * P], term[:, b * P : (b + 1) * P], True, True)
+
+        def back_gate(r):
+            for b in range(BLOCKS):
+                nc.scalar.activation(gated[r, b], turned_sums(r, b), COPY, scale=gate_turned[:, r, b : b + 1])
+                for half in range(2):
+                    first, last = r == 0 and half == 0, r == TOP - 2 and half == 1
+                    turn(back_banks[b][:, half * P : (half + 1) * P], gated[r, b][:, half * P : (half + 1) * P], first, last)
+
+        def back_finish(k):
+            t0 = FRONT + k * P
+            result = held([P, 2, P], F32, "back_result%d" % k)
+            nc.vector.tensor_tensor(result[:], last_term[:, :, t0 : t0 + P], back_banks[k][:, 0:N].rearrange("p (h t) -> p h t", h=2), ADD)
+            nc.sync.dma_start(out[:, t0 : t0 + P].rearrange("(h p) t -> p h t", h=2), result[:])
+
+        back_gather(0, 0)
+        back_gather(0, 1)
+        back_gather(1, 0)
+        back_gate(0)
+        back_gather(1, 1)
+        back_gather(2, 0)
+        back_gather(2, 1)
+        back_gate(1)
+        back_gate(2)
+        for r in range(TOP - 1):
+            front_gather(0, r)
+        front_add(0, 0)
+        last_gather(0)
+        front_add(0, 1)
+        front_gather(1, 0)
+        front_finish(0)
+        front_gather(1, 1)
+        front_gather(1, 2)
+        front_add(1, 0)
+        last_gather(1)
+        front_add(1, 1)
+        back_finish(0)
+        front_finish(1)
+        back_finish(1)
+        back_finish(2)

@@ -20,10 +20,12 @@ GELU = mybir.ActivationFunctionType.Gelu_apprx_tanh
 
 P = 128
 PASSES = K // 512
-CHUNKS = ((0, 256), (256, 256), (512, 128), (640, 128))
+PIECES = ((0, 128), (128, 256), (384, 256), (640, 128))
+CHUNKS = ((0, 0, 128), (1, 128, 256), (2, 384, 256), (3, 640, 128))
 PAIRS = E // 2
 WINDOW = 1536
-EARLY = 5
+EARLY = 4
+AFTER_GATHERS = 26624
 FRONT = 384
 BLOCKS = (T - FRONT) // P
 COPY = mybir.ActivationFunctionType.Copy
@@ -52,23 +54,23 @@ def tile_moe_sup_lin_gelu_kernel(
         pos_sb = [lists.tile([P, T // 16], U16, name="pos_sb%d" % r) for r in range(TOP)]
 
         w1_raw = held([P, PASSES, H], U32, "w1_raw")
+        w1s_rows = held([4, PASSES, 4, H], U8, "w1s_rows")
         w1s_raw = held([P, PASSES, H], U8, "w1s_raw")
-        x_sb = held([P, PASSES, T], U32, "x_sb")
+        x_sb = [held([P, PASSES, width], U32, "x_sb%d" % k) for k, (t0, width) in enumerate(PIECES)]
         xs_sb = held([P, PASSES, T], U8, "xs_sb")
         nc.vector.memset(w1s_raw[:].rearrange("p s n -> p (s n)").bitcast(I32), 0)
-        nc.vector.memset(xs_sb[:].rearrange("p s n -> p (s n)").bitcast(I32), 0)
 
-        def load_scales(plane, first, scales, r):
-            rows = scales.rearrange("s (q r) n -> r q s n", r=4)[r]
-            nc.sync.dma_start(plane[first + r : P : 32, :, :].bitcast(I32), rows.bitcast(I32))
-
-        nc.sync.dma_start(w1_raw[:].bitcast(I32), w1_words.rearrange("s p i d -> p s (i d)").bitcast(I32))
-        for r in range(4):
-            load_scales(w1s_raw, 0, w1_scales, r)
-        for r in range(4):
-            if r == 2:
-                nc.sync.dma_start(x_sb[:].bitcast(I32), x_words.rearrange("s p t d -> p s (t d)").bitcast(I32))
-            load_scales(xs_sb, 4, x_scales, r)
+        nc.sync.dma_start(w1s_rows[:].bitcast(I32), w1_scales.rearrange("s (q r) n -> r s q n", r=4).bitcast(I32))
+        for k, (t0, width) in enumerate(PIECES):
+            nc.sync.dma_start(
+                x_sb[k][:].bitcast(I32),
+                x_words[:, :, t0 : t0 + width, :].rearrange("s p t d -> p s (t d)").bitcast(I32),
+            )
+            if k == 0:
+                nc.sync.dma_start(w1_raw[:].bitcast(I32), w1_words.rearrange("s p i d -> p s (i d)").bitcast(I32))
+                for r in range(4):
+                    rows = x_scales.rearrange("s (q r) n -> r q s n", r=4)[r]
+                    nc.sync.dma_start(xs_sb[4 + r : P : 32, :, :].bitcast(I32), rows.bitcast(I32))
         w2_raw = {e: held([P, 4, N], F32, "w2_raw%d" % e, "w2_raw%d" % e) for e in range(E) if e != 4}
         w2_raw[4] = placed([P, 4, N], F32, "w2_raw4", 8192)
         for e in range(E):
@@ -90,7 +92,9 @@ def tile_moe_sup_lin_gelu_kernel(
         make_identity(nc, ident[:])
 
         w1s_sb = held([P, PASSES, H], U8, "w1s_sb")
-        w1_sb = held([P, PASSES, 4, P], U32, "w1_sb")
+        w1_sb = held([P, PASSES, 4, P], U32, "w1_sb", "w1_sb")
+        for q in range(4):
+            nc.vector.tensor_copy(w1s_raw[32 * q : 32 * q + 4, :, :].bitcast(I32), w1s_rows[:, :, q, :].bitcast(I32))
         for u in range(2):
             nc.vector.tensor_copy(
                 w1s_sb[:].rearrange("p s (j m) -> p s j m", j=4)[:, :, 2 * u : 2 * u + 2, :],
@@ -101,23 +105,25 @@ def tile_moe_sup_lin_gelu_kernel(
                 w1_raw[:].bitcast(I32).rearrange("p s (m j) -> p s j m", j=4)[:, :, 2 * u : 2 * u + 2, :],
             )
 
-        for s in range(PASSES):
+        first_words = x_sb[0][:].rearrange("p s t -> p (s t)")
+        for k in range(4):
             nc.tensor.matmul_mx(
-                out=banks[7][:],
-                lhsT=w1_raw[:, s, 0:P].bitcast(FP8X4),
-                lhsT_scale=w1s_raw[:, s, 0:P],
-                rhs=w1_raw[:, s, :].bitcast(FP8X4),
-                rhs_scale=w1s_raw[:, s, :],
+                out=banks[7][:, 0 : 2 * P],
+                lhsT=first_words[:, 0:P].bitcast(FP8X4),
+                lhsT_scale=w1s_raw[:, 0, 0:P],
+                rhs=first_words.bitcast(FP8X4),
+                rhs_scale=w1s_raw[:, 0, 0 : 2 * P],
                 start=True,
                 stop=True,
             )
 
-        h_pairs = [held([P, WINDOW], U32, "h_pairs%d" % u, "h_pairs%d" % u) for u in range(2)]
+        h_pairs = [held([P, WINDOW], U32, "h_pairs0", "h_pairs0"), placed([P, WINDOW], U32, "h_pairs1", AFTER_GATHERS)]
         for u in range(2):
             nc.vector.memset(h_pairs[u][:, T:WINDOW], 0)
         for u in range(2):
-            for k, (t0, width) in enumerate(CHUNKS):
-                acc = banks[len(CHUNKS) * u + k]
+            for k, (piece, t0, width) in enumerate(CHUNKS):
+                first = t0 - PIECES[piece][0]
+                acc = banks[((0, 1, 2, 3), (1, 2, 3, 1))[u][k]]
                 for d in range(2):
                     j = 2 * u + d
                     for s in range(PASSES):
@@ -125,7 +131,7 @@ def tile_moe_sup_lin_gelu_kernel(
                             out=acc[:, d * width : (d + 1) * width],
                             lhsT=w1_sb[:, s, j, :].bitcast(FP8X4),
                             lhsT_scale=w1s_sb[:, s, j * P : (j + 1) * P],
-                            rhs=x_sb[:, s, t0 : t0 + width].bitcast(FP8X4),
+                            rhs=x_sb[piece][:, s, first : first + width].bitcast(FP8X4),
                             rhs_scale=xs_sb[4:P, s, t0 : t0 + width],
                             start=(s == 0),
                             stop=(s == PASSES - 1),
@@ -171,7 +177,7 @@ def tile_moe_sup_lin_gelu_kernel(
 
         def cast_view(e):
             if e < EARLY:
-                return early_cast[:, e - 1, :, :].rearrange("p (h n) j -> p h n j", h=2)
+                return early_cast[e // 2][:, e % 2, :, :].rearrange("p (h n) j -> p h n j", h=2)
             return late_cast[:, :, (e - EARLY) * P : (e - EARLY + 1) * P, :]
 
         def cast_gpsimd(e):
@@ -190,14 +196,12 @@ def tile_moe_sup_lin_gelu_kernel(
         def quantize_w(e0, e1, half, offset=None):
             quantize(late_cast[:, half, (e0 - EARLY) * P : (e1 - EARLY) * P, :], [(("w", e, half), P) for e in range(e0, e1)], offset)
 
-        first_cast = held([P, N, 4], BF16, "first_cast", "w2_cast")
+        early_cast = [held([P, 2, N, 4], BF16, "early_cast%d" % g, tag) for g, tag in enumerate(("early_cast", "w1_sb"))]
+        late_cast = held([P, 2, (E - EARLY) * P, 4], BF16, "late_cast")
         nc.vector.tensor_copy(
-            first_cast[:].rearrange("p (c i) j -> p c j i", i=4),
+            early_cast[0][:, 0, :, :].rearrange("p (c i) j -> p c j i", i=4),
             w2_raw[0][:].rearrange("p j (c i) -> p c j i", i=4),
         )
-        quantize(first_cast[:], [(("w", 0, 0), P), (("w", 0, 1), P)])
-        early_cast = held([P, EARLY - 1, N, 4], BF16, "early_cast", "w2_cast")
-        late_cast = held([P, 2, (E - EARLY) * P, 4], BF16, "late_cast")
         for e in (1, 4, 5, 7, 8, 9, 10):
             cast_gpsimd(e)
         cast_scalar(2)
@@ -209,7 +213,7 @@ def tile_moe_sup_lin_gelu_kernel(
             placed([P, 2, 4 * C], U32, "picked2", 8192),
         ]
         staged = [
-            held([P, 4 * C, 4], BF16, "staged%d" % k, tag) for k, tag in enumerate(("staged0", "w2_raw6", "w2_raw11"))
+            held([P, 4 * C, 4], BF16, "staged%d" % k, tag) for k, tag in enumerate(("w2_raw3", "w2_raw6", "w2_raw11"))
         ]
 
         def slots(g0, g1):
@@ -234,34 +238,35 @@ def tile_moe_sup_lin_gelu_kernel(
         interleave_h(5, 6)
 
         def quantize_h(e0, e1):
-            quantize(staged[e0 // 4][:, e0 % 4 * C : (e0 % 4 + e1 - e0) * C, :], [(("h", e), C) for e in range(e0, e1)])
+            names = [(("h", e), C) for e in range(e0, e1)]
+            quantize(staged[e0 // 4][:, e0 % 4 * C : (e0 % 4 + e1 - e0) * C, :], names, AFTER_GATHERS + e0 * C)
 
-        def quantize_early(e0, e1, tag=""):
+        def quantize_early(e0, e1):
             names = [(("w", e, half), P) for e in range(e0, e1) for half in range(2)]
-            quantize(early_cast[:, e0 - 1 : e1 - 1, :, :].rearrange("p e n j -> p (e n) j"), names, None, tag)
+            quantize(early_cast[e0 // 2][:].rearrange("p e n j -> p (e n) j"), names, AFTER_GATHERS + S + e0 * N)
 
-        quantize_early(1, 3, "h_pairs0")
+        quantize_early(0, 2)
         quantize_h(0, 2)
         second_layer((0, 1), 0, banks[0])
         second_layer((0, 1), 1, banks[6])
         quantize_h(2, 4)
-        quantize_early(3, EARLY)
+        quantize_early(2, 4)
         second_layer((2, 3), 0, banks[1])
         second_layer((2, 3), 1, banks[7])
-        quantize_w(5, 9, 0)
+        quantize_w(4, 8, 0, AFTER_GATHERS + S + EARLY * N)
         quantize_h(4, 6)
         second_layer((4, 5), 0, banks[2])
         quantize_h(6, 8)
         second_layer((6, 7), 0, banks[3])
-        quantize_w(9, E, 0)
+        quantize_w(8, E, 0)
         quantize_h(8, 10)
         second_layer((8, 9), 0, banks[4])
         quantize_h(10, 11)
         second_layer((10,), 0, banks[5])
         quantize_h(11, E)
         second_layer((11,), 0, banks[0])
-        quantize_w(5, 9, 1, 12288)
-        quantize_w(9, E, 1, 12800)
+        quantize_w(4, 8, 1, 12288)
+        quantize_w(8, E, 1, 12800)
         for g in range(2, PAIRS):
             second_layer((2 * g, 2 * g + 1), 1, banks[g - 1])
 
@@ -272,8 +277,8 @@ def tile_moe_sup_lin_gelu_kernel(
             nc.tensor.matmul(dst, lhsT=src, rhs=ident[:], start=first, stop=last, is_transpose=True)
 
         front_terms = [held([P, TOP - 1, FRONT], F32, "front_terms%d" % half, ("picked0", "w2_raw2")[half]) for half in range(2)]
-        front_sums = [held([P, 2, FRONT], F32, "front_sums%d" % half, "w2_raw%d" % (1 + 2 * half)) for half in range(2)]
-        last_term = held([P, 2, T], F32, "last_term", "staged0")
+        front_sums = [held([P, 2, FRONT], F32, "front_sums%d" % half, "w2_raw%d" % (1 + 6 * half)) for half in range(2)]
+        last_term = held([P, 2, T], F32, "last_term", "w2_raw3")
         back_terms = {(r, half): held([P, T - FRONT], F32, "back_terms%d%d" % (r, half)) for r in range(TOP - 1) for half in range(2)}
         gated = {(r, b): held([P, N], F32, "gated%d%d" % (r, b))[:] for r in range(1, TOP - 1) for b in range(BLOCKS)}
         for b, later in enumerate(((1, 1), (2, 0), (2, 1))):

@@ -193,8 +193,8 @@ def tile_moe_sup_lin_gelu_kernel(
                 w2_raw[e][:].rearrange("p j (h c i) -> p h c j i", h=2, i=4),
             )
 
-        def quantize_w(e0, e1, half, offset=None):
-            quantize(late_cast[:, half, (e0 - EARLY) * P : (e1 - EARLY) * P, :], [(("w", e, half), P) for e in range(e0, e1)], offset)
+        def quantize_w(e0, e1, half, offset=None, tag=""):
+            quantize(late_cast[:, half, (e0 - EARLY) * P : (e1 - EARLY) * P, :], [(("w", e, half), P) for e in range(e0, e1)], offset, tag)
 
         early_cast = [held([P, 2, N, 4], BF16, "early_cast%d" % g, tag) for g, tag in enumerate(("early_cast", "w1_sb"))]
         late_cast = held([P, 2, (E - EARLY) * P, 4], BF16, "late_cast")
@@ -266,7 +266,7 @@ def tile_moe_sup_lin_gelu_kernel(
         quantize_h(11, E)
         second_layer((11,), 0, banks[0])
         quantize_w(4, 8, 1, 12288)
-        quantize_w(8, E, 1, 12800)
+        quantize_w(8, E, 1, 12800, "late_codes")
         for g in range(2, PAIRS):
             second_layer((2 * g, 2 * g + 1), 1, banks[g - 1])
 
@@ -279,16 +279,9 @@ def tile_moe_sup_lin_gelu_kernel(
         front_terms = [held([P, TOP - 1, FRONT], F32, "front_terms%d" % half, ("picked0", "w2_raw2")[half]) for half in range(2)]
         front_sums = [held([P, 2, FRONT], F32, "front_sums%d" % half, "w2_raw%d" % (1 + 6 * half)) for half in range(2)]
         last_term = held([P, 2, T], F32, "last_term", "w2_raw3")
-        back_terms = {(r, half): held([P, T - FRONT], F32, "back_terms%d%d" % (r, half)) for r in range(TOP - 1) for half in range(2)}
-        gated = {(r, b): held([P, N], F32, "gated%d%d" % (r, b))[:] for r in range(1, TOP - 1) for b in range(BLOCKS)}
-        for b, later in enumerate(((1, 1), (2, 0), (2, 1))):
-            gated[0, b] = back_terms[later][:, 0:N]
-        back_banks = (banks[3], banks[4], banks[2])
-
-        def turned_sums(r, b):
-            if b < 2:
-                return banks[(7, 0, 1)[r]][:, b * N : (b + 1) * N]
-            return banks[(6, 5, 7)[r]][:, 0:N]
+        term_tags = {(0, 0): "term_a", (1, 0): "term_b", (2, 0): "late_codes", (0, 1): "term_a", (1, 1): "term_b", (2, 1): "term_a"}
+        turned_banks = {(r, half): banks[(6, 7, 5)[r]] for r in range(TOP - 1) for half in range(2)}
+        back_banks = (banks[0], banks[1])
 
         def front_gather(half, r):
             nc.vector.tensor_tensor(front_terms[half][:, r, :], y[half][:].indirect(offsets(r, 0, FRONT)), gate_front[:, r, :], MULT)
@@ -306,33 +299,35 @@ def tile_moe_sup_lin_gelu_kernel(
             nc.vector.tensor_tensor(last_term[:, half, :], y[half][:].indirect(pos_sb[TOP - 1][:]), gate_last[:], MULT)
 
         def back_gather(r, half):
-            term = back_terms[r, half][:]
-            nc.scalar.activation(term, y[half][:].indirect(offsets(r, FRONT, T - FRONT)), COPY)
+            term = held([P, T - FRONT], F32, "back_term%d%d" % (r, half), term_tags[r, half])
+            nc.scalar.activation(term[:], y[half][:].indirect(offsets(r, FRONT, T - FRONT)), COPY)
             for b in range(BLOCKS):
-                turn(turned_sums(r, b)[:, half * P : (half + 1) * P], term[:, b * P : (b + 1) * P], True, True)
+                turn(turned_banks[r, half][:, b * P : (b + 1) * P], term[:, b * P : (b + 1) * P], True, True)
 
-        def back_gate(r):
+        def back_gate(r, half):
+            gated = held([P, T - FRONT], F32, "gated%d%d" % (r, half))
             for b in range(BLOCKS):
-                nc.scalar.activation(gated[r, b], turned_sums(r, b), COPY, scale=gate_turned[:, r, b : b + 1])
-                for half in range(2):
-                    first, last = r == 0 and half == 0, r == TOP - 2 and half == 1
-                    turn(back_banks[b][:, half * P : (half + 1) * P], gated[r, b][:, half * P : (half + 1) * P], first, last)
+                block = slice(b * P, (b + 1) * P)
+                nc.scalar.activation(gated[:, block], turned_banks[r, half][:, block], COPY, scale=gate_turned[:, r, b : b + 1])
+                turn(back_banks[half][:, block], gated[:, block], r == 0 and b == 0, r == TOP - 2 and b == BLOCKS - 1)
 
-        def back_finish(k):
-            t0 = FRONT + k * P
-            result = held([P, 2, P], F32, "back_result%d" % k)
-            nc.vector.tensor_tensor(result[:], last_term[:, :, t0 : t0 + P], back_banks[k][:, 0:N].rearrange("p (h t) -> p h t", h=2), ADD)
-            nc.sync.dma_start(out[:, t0 : t0 + P].rearrange("(h p) t -> p h t", h=2), result[:])
+        def back_finish(half):
+            result = held([P, T - FRONT], F32, "back_result%d" % half)
+            nc.vector.tensor_tensor(result[:], last_term[:, half, FRONT:T], back_banks[half][:, 0 : T - FRONT], ADD)
+            nc.sync.dma_start(out[half * P : (half + 1) * P, FRONT:T], result[:])
 
         back_gather(0, 0)
-        back_gather(0, 1)
         back_gather(1, 0)
-        back_gate(0)
-        back_gather(1, 1)
+        back_gate(0, 0)
+        back_gate(1, 0)
         back_gather(2, 0)
+        back_gather(0, 1)
+        back_gate(2, 0)
+        back_gather(1, 1)
+        back_gate(0, 1)
         back_gather(2, 1)
-        back_gate(1)
-        back_gate(2)
+        back_gate(1, 1)
+        back_gate(2, 1)
         for r in range(TOP - 1):
             front_gather(0, r)
         front_add(0, 0)
@@ -343,9 +338,8 @@ def tile_moe_sup_lin_gelu_kernel(
         front_gather(1, 1)
         front_gather(1, 2)
         front_add(1, 0)
+        back_finish(0)
         last_gather(1)
         front_add(1, 1)
-        back_finish(0)
         front_finish(1)
         back_finish(1)
-        back_finish(2)

@@ -71,8 +71,8 @@ def tile_moe_sup_lin_gelu_kernel(
                 for r in range(4):
                     rows = x_scales.rearrange("s (q r) n -> r q s n", r=4)[r]
                     nc.sync.dma_start(xs_sb[4 + r : P : 32, :, :].bitcast(I32), rows.bitcast(I32))
-        w2_raw = {e: held([P, 4, N], F32, "w2_raw%d" % e, "w2_raw%d" % e) for e in range(E) if e != 4}
-        w2_raw[4] = placed([P, 4, N], F32, "w2_raw4", 8192)
+        w2_raw = {e: held([P, 4, N], F32, "w2_raw%d" % e, "w2_raw%d" % e) for e in range(E) if e != 5}
+        w2_raw[5] = placed([P, 4, N], F32, "w2_raw5", 8192)
         for e in range(E):
             nc.sync.dma_start(w2_raw[e][:], w2[e].rearrange("(p j) n -> p j n", j=4))
             if e == 0:
@@ -202,10 +202,10 @@ def tile_moe_sup_lin_gelu_kernel(
             early_cast[0][:, 0, :, :].rearrange("p (c i) j -> p c j i", i=4),
             w2_raw[0][:].rearrange("p j (c i) -> p c j i", i=4),
         )
-        for e in (1, 4, 5, 7, 8, 9, 10):
+        for e in (1, 3, 5, 6, 8, 9, 11):
             cast_gpsimd(e)
         cast_scalar(2)
-        cast_scalar(3)
+        cast_scalar(4)
 
         picked = [
             held([P, 2, 4 * C], U32, "picked0", "picked0"),
@@ -213,7 +213,7 @@ def tile_moe_sup_lin_gelu_kernel(
             placed([P, 2, 4 * C], U32, "picked2", 8192),
         ]
         staged = [
-            held([P, 4 * C, 4], BF16, "staged%d" % k, tag) for k, tag in enumerate(("w2_raw3", "w2_raw6", "w2_raw11"))
+            held([P, 4 * C, 4], BF16, "staged%d" % k, tag) for k, tag in enumerate(("w2_raw4", "w2_raw7", "w2_raw10"))
         ]
 
         def slots(g0, g1):
@@ -231,9 +231,9 @@ def tile_moe_sup_lin_gelu_kernel(
             )
 
         interleave_h(0, 2)
-        cast_scalar(6)
+        cast_scalar(7)
         interleave_h(2, 4)
-        cast_scalar(11)
+        cast_scalar(10)
         interleave_h(4, 5)
         interleave_h(5, 6)
 
@@ -277,8 +277,8 @@ def tile_moe_sup_lin_gelu_kernel(
             nc.tensor.matmul(dst, lhsT=src, rhs=ident[:], start=first, stop=last, is_transpose=True)
 
         front_terms = [held([P, TOP - 1, FRONT], F32, "front_terms%d" % half, ("picked0", "w2_raw2")[half]) for half in range(2)]
-        front_sums = [held([P, 2, FRONT], F32, "front_sums%d" % half, "w2_raw%d" % (1 + 6 * half)) for half in range(2)]
-        last_term = held([P, 2, T], F32, "last_term", "w2_raw3")
+        front_sums = [held([P, 2, FRONT], F32, "front_sums%d" % half, "w2_raw%d" % (1 + 5 * half)) for half in range(2)]
+        last_term = held([P, 2, T], F32, "last_term", "w2_raw4")
         term_tags = {(0, 0): "term_a", (1, 0): "term_b", (2, 0): "late_codes", (0, 1): "term_a", (1, 1): "term_b", (2, 1): "term_a"}
         turned_banks = {(r, half): banks[(6, 7, 5)[r]] for r in range(TOP - 1) for half in range(2)}
         back_banks = (banks[0], banks[1])
@@ -291,7 +291,7 @@ def tile_moe_sup_lin_gelu_kernel(
             nc.vector.tensor_tensor(front_sums[half][:, k, :], first, front_terms[half][:, k + 1, :], ADD)
 
         def front_finish(half):
-            result = held([P, FRONT], F32, "front_result%d" % half, "w2_raw%d" % (5 * half))
+            result = held([P, FRONT], F32, "front_result%d" % half, "w2_raw%d" % (8 * half))
             nc.vector.tensor_tensor(result[:], last_term[:, half, 0:FRONT], front_sums[half][:, 1, :], ADD)
             nc.sync.dma_start(out[half * P : (half + 1) * P, 0:FRONT], result[:])
 

@@ -29,7 +29,7 @@ AFTER_GATHERS = 26624
 FRONT = 384
 BLOCKS = (T - FRONT) // P
 COPY = mybir.ActivationFunctionType.Copy
-GATHERS = ((0, 0, 2), (1, 0, 2), (0, 2, 4), (1, 2, 4), (0, 4, 6), (1, 4, 5), (1, 5, 6))
+GATHERS = ((0, 0, 2), (1, 0, 2), (0, 2, 4), (1, 2, 4), (0, 4, 6), (1, 4, 6))
 
 
 def tile_moe_sup_lin_gelu_kernel(
@@ -202,7 +202,7 @@ def tile_moe_sup_lin_gelu_kernel(
             early_cast[0][:, 0, :, :].rearrange("p (c i) j -> p c j i", i=4),
             w2_raw[0][:].rearrange("p j (c i) -> p c j i", i=4),
         )
-        for e in (1, 3, 5, 6, 8, 9, 11):
+        for e in range(1, E, 2):
             cast_gpsimd(e)
         cast_scalar(2)
         cast_scalar(4)
@@ -213,7 +213,7 @@ def tile_moe_sup_lin_gelu_kernel(
             placed([P, 2, 4 * C], U32, "picked2", 8192),
         ]
         staged = [
-            held([P, 4 * C, 4], BF16, "staged%d" % k, tag) for k, tag in enumerate(("w2_raw4", "w2_raw7", "w2_raw10"))
+            held([P, 4 * C, 4], BF16, "staged%d" % k, tag) for k, tag in enumerate(("w2_raw4", "w2_raw8", "w2_raw10"))
         ]
 
         def slots(g0, g1):
@@ -231,11 +231,11 @@ def tile_moe_sup_lin_gelu_kernel(
             )
 
         interleave_h(0, 2)
-        cast_scalar(7)
+        cast_scalar(6)
+        cast_scalar(8)
         interleave_h(2, 4)
         cast_scalar(10)
-        interleave_h(4, 5)
-        interleave_h(5, 6)
+        interleave_h(4, 6)
 
         def quantize_h(e0, e1):
             names = [(("h", e), C) for e in range(e0, e1)]

from contextlib import ExitStack

import concourse.mybir as mybir
from concourse.masks import make_identity

K, T, E, C, H, N, TOP = 1024, 768, 12, 256, 512, 256, 4
S = E * C
FLOPS = 2 * K * H * T + 2 * H * N * S

F32 = mybir.dt.float32
BF16 = mybir.dt.bfloat16
I32 = mybir.dt.int32
U32 = mybir.dt.uint32
U16 = mybir.dt.uint16
U8 = mybir.dt.uint8
FP8X4 = mybir.dt.float8_e4m3fn_x4
MULT = mybir.AluOpType.mult
ADD = mybir.AluOpType.add
GELU = mybir.ActivationFunctionType.Gelu_apprx_tanh

P = 128
PASSES = K // 512
PIECES = ((0, 128), (128, 256), (384, 256), (640, 128))
CHUNKS = ((0, 0, 128), (1, 128, 256), (2, 384, 256), (3, 640, 128))
PAIRS = E // 2
WINDOW = 1536
EARLY = 4
AFTER_GATHERS = 26624
FRONT = 384
BLOCKS = (T - FRONT) // P
COPY = mybir.ActivationFunctionType.Copy
GATHERS = ((0, 0, 2), (1, 0, 2), (0, 2, 4), (1, 2, 4), (0, 4, 6), (1, 4, 6))


def tile_moe_sup_lin_gelu_kernel(
    tc, x_words, x_scales, w1_words, w1_scales, w2, gate, offs, pos1, pos2, pos3, pos4, out
):
    nc = tc.nc
    with ExitStack() as ctx:
        lists = ctx.enter_context(tc.tile_pool(name="lists", bufs=1))
        keep = ctx.enter_context(tc.tile_pool(name="keep", bufs=1))
        shared = ctx.enter_context(tc.tile_pool(name="shared", bufs=1))
        psum = ctx.enter_context(tc.psum_pool(name="psum", bufs=1))

        def held(shape, dtype, name, tag=""):
            return keep.tile(shape, dtype, name=name, tag=tag, align_bytes=64)

        def placed(shape, dtype, name, offset):
            return shared.tile(shape, dtype, name=name, offset=offset, align_bytes=64)

        banks = [psum.tile([P, 512], F32, name="bank%d" % b) for b in range(8)]

        offs_sb = lists.tile([P, S // 16], U16, name="offs_sb")
        pos_sb = [lists.tile([P, T // 16], U16, name="pos_sb%d" % r) for r in range(TOP)]

        w1_raw = held([P, PASSES, H], U32, "w1_raw")
        w1s_rows = held([4, PASSES, 4, H], U8, "w1s_rows")
        w1s_raw = held([P, PASSES, H], U8, "w1s_raw")
        x_sb = [held([P, PASSES, width], U32, "x_sb%d" % k) for k, (t0, width) in enumerate(PIECES)]
        xs_sb = held([P, PASSES, T], U8, "xs_sb")
        nc.vector.memset(w1s_raw[:].rearrange("p s n -> p (s n)").bitcast(I32), 0)

        nc.sync.dma_start(w1s_rows[:].bitcast(I32), w1_scales.rearrange("s (q r) n -> r s q n", r=4).bitcast(I32))
        for k, (t0, width) in enumerate(PIECES):
            nc.sync.dma_start(
                x_sb[k][:].bitcast(I32),
                x_words[:, :, t0 : t0 + width, :].rearrange("s p t d -> p s (t d)").bitcast(I32),
            )
            if k == 0:
                nc.sync.dma_start(w1_raw[:].bitcast(I32), w1_words.rearrange("s p i d -> p s (i d)").bitcast(I32))
                for r in range(4):
                    rows = x_scales.rearrange("s (q r) n -> r q s n", r=4)[r]
                    nc.sync.dma_start(xs_sb[4 + r : P : 32, :, :].bitcast(I32), rows.bitcast(I32))
        w2_raw = {e: held([P, 4, N], F32, "w2_raw%d" % e, "w2_raw%d" % e) for e in range(E) if e != 5}
        w2_raw[5] = placed([P, 4, N], F32, "w2_raw5", 8192)
        for e in range(E):
            nc.sync.dma_start(w2_raw[e][:], w2[e].rearrange("(p j) n -> p j n", j=4))
            if e == 0:
                nc.sync.dma_start(offs_sb[:], offs)
        for r, pos in enumerate((pos1, pos2, pos3, pos4)):
            nc.sync.dma_start(pos_sb[r][:], pos)
        gate_front = held([P, TOP - 1, FRONT], F32, "gate_front")
        nc.sync.dma_start(gate_front[:], gate[0 : TOP - 1, :, 0:FRONT].rearrange("r p t -> p r t"))
        gate_last = held([P, T], F32, "gate_last")
        nc.sync.dma_start(gate_last[:], gate[TOP - 1])
        gate_turned = held([P, TOP - 1, 8], F32, "gate_turned")
        with nc.allow_non_contiguous_dma(reason="one gate value a token, a token a partition"):
            for r in range(TOP - 1):
                nc.sync.dma_start(gate_turned[:, r, 0:BLOCKS], gate[r, 0, FRONT:T].rearrange("(b p) -> p b", p=P))

        ident = held([P, P], F32, "ident")
        make_identity(nc, ident[:])

        w1s_sb = held([P, PASSES, H], U8, "w1s_sb")
        w1_sb = held([P, PASSES, 4, P], U32, "w1_sb", "w1_sb")
        for q in range(4):
            nc.vector.tensor_copy(w1s_raw[32 * q : 32 * q + 4, :, :].bitcast(I32), w1s_rows[:, :, q, :].bitcast(I32))
        for u in range(2):
            nc.vector.tensor_copy(
                w1s_sb[:].rearrange("p s (j m) -> p s j m", j=4)[:, :, 2 * u : 2 * u + 2, :],
                w1s_raw[:].rearrange("p s (m j) -> p s j m", j=4)[:, :, 2 * u : 2 * u + 2, :],
            )
            nc.vector.tensor_copy(
                w1_sb[:, :, 2 * u : 2 * u + 2, :].bitcast(I32),
                w1_raw[:].bitcast(I32).rearrange("p s (m j) -> p s j m", j=4)[:, :, 2 * u : 2 * u + 2, :],
            )

        first_words = x_sb[0][:].rearrange("p s t -> p (s t)")
        for k in range(4):
            nc.tensor.matmul_mx(
                out=banks[7][:, 0 : 2 * P],
                lhsT=first_words[:, 0:P].bitcast(FP8X4),
                lhsT_scale=w1s_raw[:, 0, 0:P],
                rhs=first_words.bitcast(FP8X4),
                rhs_scale=w1s_raw[:, 0, 0 : 2 * P],
                start=True,
                stop=True,
            )

        h_pairs = [held([P, WINDOW], U32, "h_pairs0", "h_pairs0"), placed([P, WINDOW], U32, "h_pairs1", AFTER_GATHERS)]
        for u in range(2):
            nc.vector.memset(h_pairs[u][:, T:WINDOW], 0)
        for u in range(2):
            for k, (piece, t0, width) in enumerate(CHUNKS):
                first = t0 - PIECES[piece][0]
                acc = banks[((0, 1, 2, 3), (1, 2, 3, 1))[u][k]]
                for d in range(2):
                    j = 2 * u + d
                    for s in range(PASSES):
                        nc.tensor.matmul_mx(
                            out=acc[:, d * width : (d + 1) * width],
                            lhsT=w1_sb[:, s, j, :].bitcast(FP8X4),
                            lhsT_scale=w1s_sb[:, s, j * P : (j + 1) * P],
                            rhs=x_sb[piece][:, s, first : first + width].bitcast(FP8X4),
                            rhs_scale=xs_sb[4:P, s, t0 : t0 + width],
                            start=(s == 0),
                            stop=(s == PASSES - 1),
                        )
                nc.scalar.activation(
                    h_pairs[u][:, t0 : t0 + width].bitcast(BF16).rearrange("p (t d) -> p t d", d=2),
                    acc[:, 0 : 2 * width].rearrange("p (d t) -> p t d", d=2),
                    GELU,
                )

        y = [placed([P, S], F32, "y0", 14336), placed([P, S], F32, "y1", 0)]
        quantized = {}

        def quantize(src, names, offset=None, tag=""):
            words = sum(width for name, width in names)
            label = "_".join(str(part) for part in names[0][0])
            codes = held([P, words], U32, "codes_" + label, tag)[:]
            if offset is None:
                scales = held([P, words], U8, "scales_" + label)
            else:
                scales = placed([P, words], U8, "scales_" + label, offset)
            nc.vector.quantize_mx(out=codes.bitcast(FP8X4), scales=scales[:], in_=src.rearrange("p w j -> p (w j)"))
            col = 0
            for name, width in names:
                quantized[name] = (codes[:, col : col + width], scales[:, col : col + width])
                col = col + width

        def second_layer(experts, half, bank):
            for a, e in enumerate(experts):
                w_codes, w_scales = quantized["w", e, half]
                h_codes, h_scales = quantized["h", e]
                nc.tensor.matmul_mx(
                    out=bank[:, a * C : (a + 1) * C],
                    lhsT=w_codes.bitcast(FP8X4),
                    lhsT_scale=w_scales,
                    rhs=h_codes.bitcast(FP8X4),
                    rhs_scale=h_scales,
                    start=True,
                    stop=True,
                )
            nc.scalar.copy(y[half][:, experts[0] * C : (experts[-1] + 1) * C], bank[:, 0 : len(experts) * C])


        def cast_view(e):
            if e < EARLY:
                return early_cast[e // 2][:, e % 2, :, :].rearrange("p (h n) j -> p h n j", h=2)
            return late_cast[:, :, (e - EARLY) * P : (e - EARLY + 1) * P, :]

        def cast_gpsimd(e):
            nc.gpsimd.tensor_scalar(
                cast_view(e),
                w2_raw[e][:].rearrange("p j (h n) -> p h n j", h=2),
                1.0, 0.0, MULT, ADD,
            )

        def cast_scalar(e):
            nc.scalar.copy(
                cast_view(e).rearrange("p h (c i) j -> p h c j i", i=4),
                w2_raw[e][:].rearrange("p j (h c i) -> p h c j i", h=2, i=4),
            )

        def quantize_w(e0, e1, half, offset=None, tag=""):
            quantize(late_cast[:, half, (e0 - EARLY) * P : (e1 - EARLY) * P, :], [(("w", e, half), P) for e in range(e0, e1)], offset, tag)

        early_cast = [held([P, 2, N, 4], BF16, "early_cast%d" % g, tag) for g, tag in enumerate(("early_cast", "w1_sb"))]
        late_cast = held([P, 2, (E - EARLY) * P, 4], BF16, "late_cast")
        nc.vector.tensor_copy(
            early_cast[0][:, 0, :, :].rearrange("p (c i) j -> p c j i", i=4),
            w2_raw[0][:].rearrange("p j (c i) -> p c j i", i=4),
        )
        for e in range(1, E, 2):
            cast_gpsimd(e)
        cast_scalar(2)
        cast_scalar(4)

        picked = [
            held([P, 2, 4 * C], U32, "picked0", "picked0"),
            held([P, 2, 4 * C], U32, "picked1", "w2_raw2"),
            placed([P, 2, 4 * C], U32, "picked2", 8192),
        ]
        staged = [
            held([P, 4 * C, 4], BF16, "staged%d" % k, tag) for k, tag in enumerate(("w2_raw4", "w2_raw8", "w2_raw10"))
        ]

        def slots(g0, g1):
            return slice(g0 % 2 * 2 * C, (g0 % 2 + g1 - g0) * 2 * C)

        for u, g0, g1 in GATHERS:
            nc.vector.tensor_copy(
                picked[g0 // 2][:, u, slots(g0, g1)], h_pairs[u][:].indirect(offs_sb[:, g0 * 2 * C // 16 : g1 * 2 * C // 16])
            )

        def interleave_h(g0, g1):
            nc.scalar.copy(
                staged[g0 // 2][:, slots(g0, g1), :].rearrange("p s j -> p (s j)").bitcast(F32).rearrange("p (s u) -> p s u", u=2),
                picked[g0 // 2][:, :, slots(g0, g1)].bitcast(F32).rearrange("p u s -> p s u"),
            )

        interleave_h(0, 2)
        cast_scalar(6)
        cast_scalar(8)
        interleave_h(2, 4)
        cast_scalar(10)
        interleave_h(4, 6)

        def quantize_h(e0, e1):
            names = [(("h", e), C) for e in range(e0, e1)]
            quantize(staged[e0 // 4][:, e0 % 4 * C : (e0 % 4 + e1 - e0) * C, :], names, AFTER_GATHERS + e0 * C)

        def quantize_early(e0, e1):
            names = [(("w", e, half), P) for e in range(e0, e1) for half in range(2)]
            quantize(early_cast[e0 // 2][:].rearrange("p e n j -> p (e n) j"), names, AFTER_GATHERS + S + e0 * N)

        quantize_early(0, 2)
        quantize_h(0, 2)
        second_layer((0, 1), 0, banks[0])
        second_layer((0, 1), 1, banks[6])
        quantize_h(2, 4)
        quantize_early(2, 4)
        second_layer((2, 3), 0, banks[1])
        second_layer((2, 3), 1, banks[7])
        quantize_w(4, 8, 0, AFTER_GATHERS + S + EARLY * N)
        quantize_h(4, 6)
        second_layer((4, 5), 0, banks[2])
        quantize_h(6, 8)
        second_layer((6, 7), 0, banks[3])
        quantize_w(8, E, 0)
        quantize_h(8, 10)
        second_layer((8, 9), 0, banks[4])
        quantize_h(10, 11)
        second_layer((10,), 0, banks[5])
        quantize_h(11, E)
        second_layer((11,), 0, banks[0])
        quantize_w(4, 8, 1, 12288)
        quantize_w(8, E, 1, 12800, "late_codes")
        for g in range(2, PAIRS):
            second_layer((2 * g, 2 * g + 1), 1, banks[g - 1])

        def offsets(r, t0, width):
            return pos_sb[r][:, t0 // 16 : (t0 + width) // 16]

        def turn(dst, src, first, last):
            nc.tensor.matmul(dst, lhsT=src, rhs=ident[:], start=first, stop=last, is_transpose=True)

        front_terms = [held([P, TOP - 1, FRONT], F32, "front_terms%d" % half, ("picked0", "w2_raw2")[half]) for half in range(2)]
        front_sums = [held([P, 2, FRONT], F32, "front_sums%d" % half, "w2_raw%d" % (1 + 5 * half)) for half in range(2)]
        last_term = held([P, 2, T], F32, "last_term", "w2_raw4")
        term_tags = {(0, 0): "term_a", (1, 0): "term_b", (2, 0): "late_codes", (0, 1): "term_a", (1, 1): "term_b", (2, 1): "term_a"}
        turned_banks = {(r, half): banks[(6, 7, 5)[r]] for r in range(TOP - 1) for half in range(2)}
        back_banks = (banks[0], banks[1])

        def front_gather(half, r):
            nc.vector.tensor_tensor(front_terms[half][:, r, :], y[half][:].indirect(offsets(r, 0, FRONT)), gate_front[:, r, :], MULT)

        def front_add(half, k):
            first = front_terms[half][:, 0, :] if k == 0 else front_sums[half][:, 0, :]
            nc.vector.tensor_tensor(front_sums[half][:, k, :], first, front_terms[half][:, k + 1, :], ADD)

        def front_finish(half):
            result = held([P, FRONT], F32, "front_result%d" % half, "w2_raw%d" % (8 * half))
            nc.vector.tensor_tensor(result[:], last_term[:, half, 0:FRONT], front_sums[half][:, 1, :], ADD)
            nc.sync.dma_start(out[half * P : (half + 1) * P, 0:FRONT], result[:])

        def last_gather(half):
            nc.vector.tensor_tensor(last_term[:, half, :], y[half][:].indirect(pos_sb[TOP - 1][:]), gate_last[:], MULT)

        def back_gather(r, half):
            term = held([P, T - FRONT], F32, "back_term%d%d" % (r, half), term_tags[r, half])
            nc.scalar.activation(term[:], y[half][:].indirect(offsets(r, FRONT, T - FRONT)), COPY)
            for b in range(BLOCKS):
                turn(turned_banks[r, half][:, b * P : (b + 1) * P], term[:, b * P : (b + 1) * P], True, True)

        def back_gate(r, half):
            gated = held([P, T - FRONT], F32, "gated%d%d" % (r, half))
            for b in range(BLOCKS):
                block = slice(b * P, (b + 1) * P)
                nc.scalar.activation(gated[:, block], turned_banks[r, half][:, block], COPY, scale=gate_turned[:, r, b : b + 1])
                turn(back_banks[half][:, block], gated[:, block], r == 0 and b == 0, r == TOP - 2 and b == BLOCKS - 1)

        def back_finish(half):
            result = held([P, T - FRONT], F32, "back_result%d" % half)
            nc.vector.tensor_tensor(result[:], last_term[:, half, FRONT:T], back_banks[half][:, 0 : T - FRONT], ADD)
            nc.sync.dma_start(out[half * P : (half + 1) * P, FRONT:T], result[:])

        back_gather(0, 0)
        back_gather(1, 0)
        back_gate(0, 0)
        back_gate(1, 0)
        back_gather(2, 0)
        back_gather(0, 1)
        back_gate(2, 0)
        back_gather(1, 1)
        back_gate(0, 1)
        back_gather(2, 1)
        back_gate(1, 1)
        back_gate(2, 1)
        for r in range(TOP - 1):
            front_gather(0, r)
        front_add(0, 0)
        last_gather(0)
        front_add(0, 1)
        front_gather(1, 0)
        front_finish(0)
        front_gather(1, 1)
        front_gather(1, 2)
        front_add(1, 0)
        back_finish(0)
        last_gather(1)
        front_add(1, 1)
        front_finish(1)
        back_finish(1)
